import numpy as np
import ml_dtypes


def mxq(x, axis, fmt="e4m3"):
    dtype, down = {"e4m3": (ml_dtypes.float8_e4m3fn, 7), "e5m2": (ml_dtypes.float8_e5m2, 14)}[fmt]
    v = np.moveaxis(np.asarray(x, np.float32).astype(ml_dtypes.bfloat16).astype(np.float64), axis, -1)
    blocks = v.reshape(v.shape[:-1] + (-1, 32))
    amax = np.abs(blocks).max(-1, keepdims=True)
    byte = np.maximum(np.where(amax > 0, np.frexp(amax)[1] - 1 + 127, 0) - down, 1)
    scale = np.exp2(byte - 127.0)
    codes = (blocks / scale).astype(np.float32).astype(dtype).astype(np.float64)
    return np.moveaxis((codes * scale).reshape(v.shape), -1, axis)


WIDE = False


def mx_kscale(k):
    if not WIDE:
        return np.ones(k)
    levels = np.array([10, -10, 5, -5, 0])
    if k % 512:
        return np.exp2(np.random.permutation(np.resize(levels, k // 32))).repeat(32)
    a = np.empty((k // 512, 16))
    for p in range(k // 512):
        a[p, :8] = np.random.permutation(np.resize(levels, 8))
        for g in range(8):
            far = levels[np.abs(levels - a[p, g]) >= 10]
            a[p, g + 8] = far[np.random.randint(len(far))]
    return np.exp2(a.ravel()).repeat(32)


def f64(x):
    return np.asarray(x).astype(np.float64)


def striped(idx):
    return np.tile(idx.reshape(-1, 16).T, (8, 1)).astype(np.uint16)


def unstriped(offs):
    return offs[:16].T.reshape(-1).astype(np.int64)


K, T, E, C, N = 1024, 1280, 8, 128, 512
M = 384


def by_expert(wq, xq):
    return np.concatenate([wq[e].T @ xq[:, e * C:(e + 1) * C] for e in range(E)], axis=1)


def setup_inputs():
    n = np.random.standard_normal
    s = mx_kscale(K)[:, None]
    v = mx_kscale(N)
    return {
        "xT": (n((K, T)) * s).astype(np.float32),
        "w": (n((E, K, N)) / np.sqrt(K) / s[None] * v[None, None, :]).astype(np.float32),
        "wp": (n((N, M)) / np.sqrt(N) / v[:, None]).astype(np.float32),
        "gate": np.tile(np.random.uniform(0.2, 1.0, E * C), (N, 1)).astype(np.float32),
        "offs": striped(np.random.permutation(T)[:E * C]),
    }


def reference(xT, w, wp, gate, offs):
    idx = unstriped(offs)
    xq = mxq(f64(xT)[:, idx], 0, "e4m3")
    y = by_expert(mxq(f64(w), 1, "e4m3"), xq)
    c = np.zeros((N, T))
    c[:, idx] = f64(gate) * y
    return mxq(f64(wp), 0, "e4m3").T @ mxq(c, 0, "e4m3")

@@ -1,0 +1,365 @@
+from contextlib import ExitStack
+
+import concourse.mybir as mybir
+
+K, T, E, C, N, M = 1024, 1280, 8, 128, 512, 384
+SLOTS = E * C
+FLOPS = 2 * SLOTS * K * N + 2 * T * N * M
+BYTES = 4 * (K * T + E * K * N + N * M + SLOTS + M * T) + 2 * SLOTS
+
+F32 = mybir.dt.float32
+BF16 = mybir.dt.bfloat16
+U32 = mybir.dt.uint32
+U16 = mybir.dt.uint16
+U8 = mybir.dt.uint8
+FP8X4 = mybir.dt.float8_e4m3fn_x4
+ADD = mybir.AluOpType.add
+MULT = mybir.AluOpType.mult
+COPY = mybir.ActivationFunctionType.Copy
+
+P = 128
+PACK = 4
+KP = P * PACK
+PASSES = K // KP
+GATHER = 512
+XRAW, XBF, WRAW, WBF, WQ = 4, 3, 5, 4, 4
+X_CHUNKS = ((0, 0, 256), (0, 256, 768), (0, 768, 1280), (1, 0, 512), (1, 512, 1024), (1, 1024, 1280))
+X_ENGINE = 'vvsvsv'
+W_ENGINE = 'ssssssssssssssss'
+WP_ENGINE = 's'
+LAST_ENGINE = 'sssssssssssssss'
+GROUPS = ((0, 2), (2, 2), (4, 2), (6, 1), (7, 1))
+CUTS = ((0, 256), (256, 512), (512, 704), (704, 864), (864, 1024))
+TURN_ENGINE = 'ssssssss'
+SPLIT = {"p": 192, "q": 128, "r": 256}
+GROUP_OF = {0: (0, 0, 2), 1: (0, 0, 2), 2: (1, 2, 2), 3: (1, 2, 2), 4: (2, 4, 2), 5: (2, 4, 2), 6: (3, 6, 1), 7: (4, 7, 1)}
+
+
+def tile_moe_nxt_lin_none_kernel(tc, xT, w, wp, gate, offs, out):
+    nc = tc.nc
+    with ExitStack() as ctx:
+        keep = ctx.enter_context(tc.tile_pool(name="keep", bufs=1))
+        xraw = ctx.enter_context(tc.tile_pool(name="xraw", bufs=XRAW))
+        xbf = ctx.enter_context(tc.tile_pool(name="xbf", bufs=XBF))
+        wraw = ctx.enter_context(tc.tile_pool(name="wraw", bufs=WRAW))
+        wbf = ctx.enter_context(tc.tile_pool(name="wbf", bufs=WBF))
+        wq = ctx.enter_context(tc.tile_pool(name="wq", bufs=WQ))
+        cpool = ctx.enter_context(tc.tile_pool(name="c", bufs=2))
+        ypsum = ctx.enter_context(tc.psum_pool(name="ypsum", bufs=3))
+        opsum = ctx.enter_context(tc.psum_pool(name="opsum", bufs=2))
+
+        offsets = keep.tile([P, SLOTS // 16], U16, name="offsets")
+        nc.sync.dma_start(offsets[:], offs)
+
+        xcodes = [keep.tile([P, T], U32, align_bytes=64, name="xcodes%d" % a) for a in range(PASSES)]
+        xscales = keep.tile([P, T], U8, align_bytes=64, name="xscales")
+        gcodes = [keep.tile([P, SLOTS], U32, align_bytes=64, name="gcodes%d" % a) for a in range(PASSES)]
+        gscales = keep.tile([P, SLOTS], U8, align_bytes=64, name="gscales")
+        gates = keep.tile([P, SLOTS], F32, name="gates")
+        wpraw = keep.tile([P, PACK, M], F32, name="wpraw")
+        wpbf = keep.tile([P, M, PACK], BF16, align_bytes=64, name="wpbf")
+        wpcodes = keep.tile([P, M], U32, align_bytes=64, name="wpcodes")
+        wpscales = keep.tile([P, M], U8, align_bytes=64, name="wpscales")
+        oslots = [keep.tile([P, SLOTS], F32, name="oslots%d" % f) for f in range(M // P)]
+        windows = [keep.tile([P, T], F32, name="window%d" % f) for f in range(M // P)]
+
+        nc.gpsimd.memset(xscales[:], 0)
+        for f in range(M // P):
+            nc.gpsimd.memset(windows[f][:], 0.0)
+
+        x_tiles = {}
+        x_parts = {}
+        raw_tiles = {}
+        grouped_tiles = {}
+        quantized = {}
+        products = {}
+        gated = {}
+        ccodes_of = {}
+        projected = {}
+
+        def copy(engine, dst, src):
+            if engine == "v":
+                nc.vector.tensor_copy(out=dst, in_=src)
+            elif engine == "g":
+                nc.gpsimd.tensor_scalar(out=dst, in0=src, scalar1=1.0, scalar2=0.0, op0=MULT, op1=ADD)
+            else:
+                nc.scalar.activation(out=dst, in_=src, func=COPY)
+
+        def LX(i):
+            a, t0, t1 = X_CHUNKS[i]
+            xr = xraw.tile([P, PACK, t1 - t0], F32, name="xr")
+            nc.sync.dma_start(xr[:], xT[a * KP:(a + 1) * KP, t0:t1].rearrange("(p j) t -> p j t", j=PACK))
+            x_parts[i] = xr
+
+        def GX(i):
+            a, t0, t1 = X_CHUNKS[i]
+            xb = xbf.tile([P, (t1 - t0) * PACK], BF16, align_bytes=64, name="xb")
+            copy(
+                X_ENGINE[i],
+                xb[:].rearrange("p (c i j) -> p c j i", i=4, j=PACK),
+                x_parts.pop(i)[:].rearrange("p j (c i) -> p c j i", i=4),
+            )
+            x_tiles[i] = xb
+
+        def QX(i):
+            a, t0, t1 = X_CHUNKS[i]
+            nc.vector.quantize_mx(
+                out=xcodes[a][:, t0:t1].bitcast(FP8X4), scales=xscales[PACK * a:P, t0:t1], in_=x_tiles.pop(i)[:]
+            )
+
+        def GA(a, g):
+            nc.vector.tensor_copy(
+                out=gcodes[a][:, g * GATHER:(g + 1) * GATHER],
+                in_=xcodes[a][:].indirect(offsets[:, g * GATHER // 16:(g + 1) * GATHER // 16]),
+            )
+
+        def GS(g):
+            nc.vector.tensor_copy(
+                out=gscales[:, g * GATHER:(g + 1) * GATHER],
+                in_=xscales[:].indirect(offsets[:, g * GATHER // 16:(g + 1) * GATHER // 16]),
+            )
+
+        def LG():
+            nc.sync.dma_start(gates[:], gate[0:P, :])
+
+        def LP():
+            nc.sync.dma_start(wpraw[:], wp.rearrange("(q r) f -> q r f", r=PACK))
+
+        def GP():
+            copy(
+                WP_ENGINE,
+                wpbf[:].rearrange("q (c i) r -> q c r i", i=4),
+                wpraw[:].rearrange("q r (c i) -> q c r i", i=4),
+            )
+
+        def QP(i):
+            f0, f1 = ((0, 256), (256, 384))[i]
+            nc.vector.quantize_mx(
+                out=wpcodes[:, f0:f1].bitcast(FP8X4),
+                scales=wpscales[:, f0:f1],
+                in_=wpbf[:, f0:f1, :].rearrange("p f r -> p (f r)"),
+            )
+
+        def LW(k):
+            e, a = divmod(k, PASSES)
+            raw = wraw.tile([P, PACK, N], F32, name="raw")
+            nc.sync.dma_start(raw[:], w[e, a * KP:(a + 1) * KP, :].rearrange("(p j) n -> p j n", j=PACK))
+            raw_tiles[k] = raw
+
+        def GW(k):
+            grouped = wbf.tile([P, N * PACK], BF16, align_bytes=64, name="grouped")
+            dst = grouped[:].rearrange("p (t m j) -> p m j t", t=PACK, j=PACK)
+            src = raw_tiles.pop(k)[:].rearrange("p j (m t) -> p m j t", t=PACK)
+            copy(W_ENGINE[k], dst, src)
+            grouped_tiles[k] = grouped
+
+        def QW(k):
+            codes = wq.tile([P, N], U32, align_bytes=64, name="codes")
+            scales = wq.tile([P, N], U8, align_bytes=64, name="scales")
+            nc.vector.quantize_mx(out=codes[:].bitcast(FP8X4), scales=scales[:], in_=grouped_tiles.pop(k)[:])
+            quantized[k] = codes, scales
+
+        def MM(e):
+            y = ypsum.tile([P, PACK, C], F32, name="y")
+            for t in range(PACK):
+                for a in range(PASSES):
+                    codes, scales = quantized[e * PASSES + a]
+                    nc.tensor.matmul_mx(
+                        out=y[:, t, :],
+                        lhsT=codes[:, t * P:(t + 1) * P].bitcast(FP8X4),
+                        lhsT_scale=scales[:, t * P:(t + 1) * P],
+                        rhs=gcodes[a][:, e * C:(e + 1) * C].bitcast(FP8X4),
+                        rhs_scale=gscales[PACK * a:P, e * C:(e + 1) * C],
+                        start=(a == 0),
+                        stop=(a == PASSES - 1),
+                    )
+            products[e] = y
+
+        def GT(e):
+            gi, first, size = GROUP_OF[e]
+            if gi not in gated:
+                cb = cpool.tile([P, size * C, PACK], BF16, align_bytes=64, name="cb")
+                gated[gi] = cb
+            i = e - first
+            nc.vector.tensor_tensor(
+                out=gated[gi][:, i * C:(i + 1) * C, :],
+                in0=products.pop(e)[:].rearrange("p t s -> p s t"),
+                in1=gates[:, e * C:(e + 1) * C].unsqueeze(2).to_broadcast([P, C, PACK]),
+                op=MULT,
+            )
+
+        def QC(gi):
+            width = GROUPS[gi][1] * C
+            ccodes = cpool.tile([P, width], U32, align_bytes=64, name="ccodes")
+            cscales = cpool.tile([P, width], U8, align_bytes=64, name="cscales")
+            nc.vector.quantize_mx(
+                out=ccodes[:].bitcast(FP8X4), scales=cscales[:], in_=gated[gi][:].rearrange("p s r -> p (s r)")
+            )
+            ccodes_of[gi] = ccodes, cscales
+
+        def PM(gi):
+            width = GROUPS[gi][1] * C
+            ccodes, cscales = ccodes_of.pop(gi)
+            o = opsum.tile([P, 4, 2 * C], F32, name="o")
+            for f in range(M // P):
+                nc.tensor.matmul_mx(
+                    out=o[:, f, 0:width],
+                    lhsT=wpcodes[:, f * P:(f + 1) * P].bitcast(FP8X4),
+                    lhsT_scale=wpscales[:, f * P:(f + 1) * P],
+                    rhs=ccodes[:].bitcast(FP8X4),
+                    rhs_scale=cscales[:],
+                    start=True,
+                    stop=True,
+                )
+            projected[gi] = o
+
+        def EV(gi, f):
+            first, size = GROUPS[gi]
+            s0, s1 = first * C, (first + size) * C
+            copy(LAST_ENGINE[gi * 3 + f], oslots[f][:, s0:s1], projected[gi][:, f, 0:s1 - s0])
+
+        def SC(i, f):
+            a0, a1 = CUTS[i]
+            nc.vector.tensor_copy(
+                out=windows[f][:].indirect(offsets[:, a0 // 16:a1 // 16]), in_=oslots[f][:, a0:a1]
+            )
+
+        def ST(f):
+            nc.sync.dma_start(out[f * P:(f + 1) * P, :], windows[f][:])
+
+        LX(0)
+        GX(0)
+        QX(0)
+        LX(2)
+        GX(2)
+        QX(2)
+        LX(1)
+        GX(1)
+        QX(1)
+        GA(0, 0)
+        GA(0, 1)
+        LX(4)
+        GX(4)
+        QX(4)
+        LX(3)
+        GX(3)
+        QX(3)
+        LW(0)
+        GW(0)
+        LX(5)
+        GX(5)
+        QX(5)
+        GA(1, 0)
+        GA(1, 1)
+        LW(1)
+        LG()
+        LP()
+        LW(2)
+        LW(3)
+        LW(4)
+        GS(0)
+        GS(1)
+        GW(1)
+        QW(0)
+        QW(1)
+        GW(2)
+        GW(3)
+        LW(5)
+        GP()
+        QP(0)
+        QP(1)
+        MM(0)
+        GT(0)
+        QW(2)
+        QW(3)
+        GW(4)
+        LW(6)
+        GW(5)
+        LW(7)
+        MM(1)
+        GT(1)
+        QW(4)
+        QW(5)
+        QC(0)
+        PM(0)
+        EV(0, 0)
+        EV(0, 1)
+        EV(0, 2)
+        GW(6)
+        LW(8)
+        GW(7)
+        LW(9)
+        MM(2)
+        GT(2)
+        QW(6)
+        QW(7)
+        GW(8)
+        LW(10)
+        GW(9)
+        LW(11)
+        MM(3)
+        GT(3)
+        QW(8)
+        QW(9)
+        QC(1)
+        PM(1)
+        EV(1, 0)
+        EV(1, 1)
+        EV(1, 2)
+        GW(10)
+        LW(12)
+        GW(11)
+        LW(13)
+        MM(4)
+        GT(4)
+        QW(10)
+        QW(11)
+        SC(0, 0)
+        SC(0, 1)
+        SC(0, 2)
+        GW(12)
+        LW(14)
+        GW(13)
+        LW(15)
+        MM(5)
+        GT(5)
+        QW(12)
+        QW(13)
+        QC(2)
+        PM(2)
+        EV(2, 0)
+        EV(2, 1)
+        EV(2, 2)
+        GW(14)
+        GW(15)
+        MM(6)
+        GT(6)
+        QW(14)
+        QW(15)
+        QC(3)
+        PM(3)
+        EV(3, 0)
+        EV(3, 1)
+        EV(3, 2)
+        MM(7)
+        GT(7)
+        QC(4)
+        PM(4)
+        EV(4, 0)
+        EV(4, 1)
+        EV(4, 2)
+        SC(1, 0)
+        SC(1, 1)
+        SC(1, 2)
+        SC(2, 0)
+        SC(2, 1)
+        SC(2, 2)
+        SC(3, 0)
+        SC(3, 1)
+        SC(3, 2)
+        SC(4, 0)
+        SC(4, 1)
+        SC(4, 2)
+        ST(0)
+        ST(1)
+        ST(2)

@@ -9,6 +9,7 @@ BYTES = 4 * (K * T + E * K * N + N * M + SLOTS + M * T) + 2 * SLOTS
 
 F32 = mybir.dt.float32
 BF16 = mybir.dt.bfloat16
+I32 = mybir.dt.int32
 U32 = mybir.dt.uint32
 U16 = mybir.dt.uint16
 U8 = mybir.dt.uint8
@@ -21,31 +22,29 @@ P = 128
 PACK = 4
 KP = P * PACK
 PASSES = K // KP
-GATHER = 512
-XRAW, XBF, WRAW, WBF, WQ = 4, 3, 5, 4, 4
-X_CHUNKS = ((0, 0, 256), (0, 256, 768), (0, 768, 1280), (1, 0, 512), (1, 512, 1024), (1, 1024, 1280))
-X_ENGINE = 'vvsvsv'
-W_ENGINE = 'ssssssssssssssss'
-WP_ENGINE = 's'
-LAST_ENGINE = 'sssssssssssssss'
-GROUPS = ((0, 2), (2, 2), (4, 2), (6, 1), (7, 1))
-CUTS = ((0, 256), (256, 512), (512, 704), (704, 864), (864, 1024))
-TURN_ENGINE = 'ssssssss'
-SPLIT = {"p": 192, "q": 128, "r": 256}
-GROUP_OF = {0: (0, 0, 2), 1: (0, 0, 2), 2: (1, 2, 2), 3: (1, 2, 2), 4: (2, 4, 2), 5: (2, 4, 2), 6: (3, 6, 1), 7: (4, 7, 1)}
+HALVES = 2
+F_BLOCKS = M // P
+X_CHUNKS = ((0, 0, 512, "s"), (0, 512, 1024, "v"), (0, 1024, 1280, "s"), (1, 0, 512, "s"), (1, 512, 1024, "v"), (1, 1024, 1280, "s"))
+GATHERS = ((0, 256), (256, 640), (640, 1024))
+CUTS = ((0, 192), (192, 384), (384, 576), (576, 768), (768, 1024))
+VECTOR_SHARE = (0, 0, 0, 0, 0, 0, 0, 0, 0, 0, 0, 0, 0, 0, 0, 64)
+BLOCK = 256
+ZEROS = T // BLOCK
+TOKEN_CHUNKS = ((0, 256), (256, 512), (512, 768), (768, 1024), (1024, 1152), (1152, 1280))
 
 
 def tile_moe_nxt_lin_none_kernel(tc, xT, w, wp, gate, offs, out):
     nc = tc.nc
     with ExitStack() as ctx:
         keep = ctx.enter_context(tc.tile_pool(name="keep", bufs=1))
-        xraw = ctx.enter_context(tc.tile_pool(name="xraw", bufs=XRAW))
-        xbf = ctx.enter_context(tc.tile_pool(name="xbf", bufs=XBF))
-        wraw = ctx.enter_context(tc.tile_pool(name="wraw", bufs=WRAW))
-        wbf = ctx.enter_context(tc.tile_pool(name="wbf", bufs=WBF))
-        wq = ctx.enter_context(tc.tile_pool(name="wq", bufs=WQ))
-        cpool = ctx.enter_context(tc.tile_pool(name="c", bufs=2))
-        ypsum = ctx.enter_context(tc.psum_pool(name="ypsum", bufs=3))
+        xraw = ctx.enter_context(tc.tile_pool(name="xraw", bufs=6))
+        xbf = ctx.enter_context(tc.tile_pool(name="xbf", bufs=3))
+        wraw = ctx.enter_context(tc.tile_pool(name="wraw", bufs=6))
+        wbf = ctx.enter_context(tc.tile_pool(name="wbf", bufs=4))
+        wq = ctx.enter_context(tc.tile_pool(name="wq", bufs=5))
+        cpool = ctx.enter_context(tc.tile_pool(name="c", bufs=3))
+        opool = ctx.enter_context(tc.tile_pool(name="o", bufs=len(TOKEN_CHUNKS)))
+        ypsum = ctx.enter_context(tc.psum_pool(name="ypsum", bufs=2))
         opsum = ctx.enter_context(tc.psum_pool(name="opsum", bufs=2))
 
         offsets = keep.tile([P, SLOTS // 16], U16, name="offsets")
@@ -55,155 +54,143 @@ def tile_moe_nxt_lin_none_kernel(tc, xT, w, wp, gate, offs, out):
         xscales = keep.tile([P, T], U8, align_bytes=64, name="xscales")
         gcodes = [keep.tile([P, SLOTS], U32, align_bytes=64, name="gcodes%d" % a) for a in range(PASSES)]
         gscales = keep.tile([P, SLOTS], U8, align_bytes=64, name="gscales")
-        gates = keep.tile([P, SLOTS], F32, name="gates")
+        gates = {}
         wpraw = keep.tile([P, PACK, M], F32, name="wpraw")
         wpbf = keep.tile([P, M, PACK], BF16, align_bytes=64, name="wpbf")
         wpcodes = keep.tile([P, M], U32, align_bytes=64, name="wpcodes")
         wpscales = keep.tile([P, M], U8, align_bytes=64, name="wpscales")
-        oslots = [keep.tile([P, SLOTS], F32, name="oslots%d" % f) for f in range(M // P)]
-        windows = [keep.tile([P, T], F32, name="window%d" % f) for f in range(M // P)]
+        pairs = [keep.tile([P, SLOTS * 2], BF16, align_bytes=64, name="pairs%d" % u) for u in range(HALVES)]
+        windows = [keep.tile([P, T + BLOCK], F32, name="window%d" % u) for u in range(HALVES)]
 
-        nc.gpsimd.memset(xscales[:], 0)
-        for f in range(M // P):
-            nc.gpsimd.memset(windows[f][:], 0.0)
-
-        x_tiles = {}
-        x_parts = {}
-        raw_tiles = {}
-        grouped_tiles = {}
-        quantized = {}
-        products = {}
-        gated = {}
-        ccodes_of = {}
-        projected = {}
+        nc.vector.memset(xscales[:].bitcast(I32), 0)
+        for u in range(HALVES):
+            nc.vector.memset(windows[u][:], 0.0)
 
         def copy(engine, dst, src):
             if engine == "v":
                 nc.vector.tensor_copy(out=dst, in_=src)
-            elif engine == "g":
-                nc.gpsimd.tensor_scalar(out=dst, in0=src, scalar1=1.0, scalar2=0.0, op0=MULT, op1=ADD)
             else:
                 nc.scalar.activation(out=dst, in_=src, func=COPY)
 
-        def LX(i):
-            a, t0, t1 = X_CHUNKS[i]
+        def offsets_of(s0, s1):
+            return offsets[:, s0 // 16:s1 // 16]
+
+        def load_x(a, t0, t1):
             xr = xraw.tile([P, PACK, t1 - t0], F32, name="xr")
             nc.sync.dma_start(xr[:], xT[a * KP:(a + 1) * KP, t0:t1].rearrange("(p j) t -> p j t", j=PACK))
-            x_parts[i] = xr
+            return xr
 
-        def GX(i):
-            a, t0, t1 = X_CHUNKS[i]
+        def quantize_x(xr, a, t0, t1, engine):
             xb = xbf.tile([P, (t1 - t0) * PACK], BF16, align_bytes=64, name="xb")
             copy(
-                X_ENGINE[i],
+                engine,
                 xb[:].rearrange("p (c i j) -> p c j i", i=4, j=PACK),
-                x_parts.pop(i)[:].rearrange("p j (c i) -> p c j i", i=4),
+                xr[:].rearrange("p j (c i) -> p c j i", i=4),
             )
-            x_tiles[i] = xb
-
-        def QX(i):
-            a, t0, t1 = X_CHUNKS[i]
             nc.vector.quantize_mx(
-                out=xcodes[a][:, t0:t1].bitcast(FP8X4), scales=xscales[PACK * a:P, t0:t1], in_=x_tiles.pop(i)[:]
+                out=xcodes[a][:, t0:t1].bitcast(FP8X4), scales=xscales[PACK * a:P, t0:t1], in_=xb[:]
             )
 
-        def GA(a, g):
-            nc.vector.tensor_copy(
-                out=gcodes[a][:, g * GATHER:(g + 1) * GATHER],
-                in_=xcodes[a][:].indirect(offsets[:, g * GATHER // 16:(g + 1) * GATHER // 16]),
-            )
+        def gather_codes(a, s0, s1):
+            nc.vector.tensor_copy(out=gcodes[a][:, s0:s1], in_=xcodes[a][:].indirect(offsets_of(s0, s1)))
 
-        def GS(g):
-            nc.vector.tensor_copy(
-                out=gscales[:, g * GATHER:(g + 1) * GATHER],
-                in_=xscales[:].indirect(offsets[:, g * GATHER // 16:(g + 1) * GATHER // 16]),
-            )
+        def gather_scales(s0, s1):
+            nc.vector.tensor_copy(out=gscales[:, s0:s1], in_=xscales[:].indirect(offsets_of(s0, s1)))
 
-        def LG():
-            nc.sync.dma_start(gates[:], gate[0:P, :])
-
-        def LP():
-            nc.sync.dma_start(wpraw[:], wp.rearrange("(q r) f -> q r f", r=PACK))
-
-        def GP():
-            copy(
-                WP_ENGINE,
-                wpbf[:].rearrange("q (c i) r -> q c r i", i=4),
-                wpraw[:].rearrange("q r (c i) -> q c r i", i=4),
-            )
-
-        def QP(i):
-            f0, f1 = ((0, 256), (256, 384))[i]
-            nc.vector.quantize_mx(
-                out=wpcodes[:, f0:f1].bitcast(FP8X4),
-                scales=wpscales[:, f0:f1],
-                in_=wpbf[:, f0:f1, :].rearrange("p f r -> p (f r)"),
-            )
-
-        def LW(k):
+        def load_w(k):
             e, a = divmod(k, PASSES)
             raw = wraw.tile([P, PACK, N], F32, name="raw")
             nc.sync.dma_start(raw[:], w[e, a * KP:(a + 1) * KP, :].rearrange("(p j) n -> p j n", j=PACK))
-            raw_tiles[k] = raw
+            return raw
 
-        def GW(k):
+        def quantize_w(k, raw):
             grouped = wbf.tile([P, N * PACK], BF16, align_bytes=64, name="grouped")
             dst = grouped[:].rearrange("p (t m j) -> p m j t", t=PACK, j=PACK)
-            src = raw_tiles.pop(k)[:].rearrange("p j (m t) -> p m j t", t=PACK)
-            copy(W_ENGINE[k], dst, src)
-            grouped_tiles[k] = grouped
-
-        def QW(k):
+            src = raw[:].rearrange("p j (m t) -> p m j t", t=PACK)
+            split = P - VECTOR_SHARE[k]
+            copy("s", dst[:, 0:split], src[:, 0:split])
+            if split < P:
+                copy("v", dst[:, split:P], src[:, split:P])
             codes = wq.tile([P, N], U32, align_bytes=64, name="codes")
             scales = wq.tile([P, N], U8, align_bytes=64, name="scales")
-            nc.vector.quantize_mx(out=codes[:].bitcast(FP8X4), scales=scales[:], in_=grouped_tiles.pop(k)[:])
-            quantized[k] = codes, scales
+            nc.vector.quantize_mx(out=codes[:].bitcast(FP8X4), scales=scales[:], in_=grouped[:])
+            return codes, scales
 
-        def MM(e):
-            y = ypsum.tile([P, PACK, C], F32, name="y")
-            for t in range(PACK):
-                for a in range(PASSES):
-                    codes, scales = quantized[e * PASSES + a]
-                    nc.tensor.matmul_mx(
-                        out=y[:, t, :],
-                        lhsT=codes[:, t * P:(t + 1) * P].bitcast(FP8X4),
-                        lhsT_scale=scales[:, t * P:(t + 1) * P],
-                        rhs=gcodes[a][:, e * C:(e + 1) * C].bitcast(FP8X4),
-                        rhs_scale=gscales[PACK * a:P, e * C:(e + 1) * C],
-                        start=(a == 0),
-                        stop=(a == PASSES - 1),
-                    )
-            products[e] = y
+        def expert(e, quantized):
+            cols = slice(e * C, (e + 1) * C)
+            for u in range(HALVES):
+                y = ypsum.tile([P, 2, C], F32, name="y%d" % u)
+                for i in range(2):
+                    t = 2 * u + i
+                    for a in range(PASSES):
+                        codes, scales = quantized[a]
+                        nc.tensor.matmul_mx(
+                            out=y[:, i, :],
+                            lhsT=codes[:, t * P:(t + 1) * P].bitcast(FP8X4),
+                            lhsT_scale=scales[:, t * P:(t + 1) * P],
+                            rhs=gcodes[a][:, cols].bitcast(FP8X4),
+                            rhs_scale=gscales[PACK * a:P, cols],
+                            start=(a == 0),
+                            stop=(a == PASSES - 1),
+                        )
+                nc.vector.tensor_tensor(
+                    out=pairs[u][:, 2 * e * C:2 * (e + 1) * C].rearrange("p (s i) -> p s i", i=2),
+                    in0=y[:].rearrange("p i s -> p s i"),
+                    in1=gates[e].unsqueeze(2).to_broadcast([P, C, 2]),
+                    op=MULT,
+                )
 
-        def GT(e):
-            gi, first, size = GROUP_OF[e]
-            if gi not in gated:
-                cb = cpool.tile([P, size * C, PACK], BF16, align_bytes=64, name="cb")
-                gated[gi] = cb
-            i = e - first
-            nc.vector.tensor_tensor(
-                out=gated[gi][:, i * C:(i + 1) * C, :],
-                in0=products.pop(e)[:].rearrange("p t s -> p s t"),
-                in1=gates[:, e * C:(e + 1) * C].unsqueeze(2).to_broadcast([P, C, PACK]),
-                op=MULT,
+        def load_gates(e0, e1):
+            tile = keep.tile([P, (e1 - e0) * C], F32, name="gates%d" % e0)
+            nc.sync.dma_start(tile[:], gate[0:P, e0 * C:e1 * C])
+            for e in range(e0, e1):
+                gates[e] = tile[:, (e - e0) * C:(e - e0 + 1) * C]
+
+        def scatter(s0, s1):
+            for u in range(HALVES):
+                nc.vector.tensor_copy(
+                    out=windows[u][:].indirect(offsets_of(s0, s1)), in_=pairs[u][:, 2 * s0:2 * s1].bitcast(F32)
+                )
+
+        def quantize_wp():
+            copy(
+                "s",
+                wpbf[:].rearrange("q (c i) r -> q c r i", i=4),
+                wpraw[:].rearrange("q r (c i) -> q c r i", i=4),
             )
+            for f0, f1 in ((0, 256), (256, M)):
+                nc.vector.quantize_mx(
+                    out=wpcodes[:, f0:f1].bitcast(FP8X4),
+                    scales=wpscales[:, f0:f1],
+                    in_=wpbf[:, f0:f1, :].rearrange("p f r -> p (f r)"),
+                )
 
-        def QC(gi):
-            width = GROUPS[gi][1] * C
+        def weave(t0, t1):
+            woven = cpool.tile([P, (t1 - t0) * PACK], BF16, align_bytes=64, name="woven")
+            b = t0 // BLOCK
+            picks = (slice(b, ZEROS + 1, ZEROS - b), slice(ZEROS, b - 1 if b else None, b - ZEROS))
+            halves = [
+                windows[u][:]
+                .bitcast(BF16)
+                .rearrange("p (b s i) -> p b s i", s=BLOCK, i=2)[:, picks[u], t0 - b * BLOCK:t1 - b * BLOCK, :]
+                .rearrange("p u s i -> p s u i")
+                for u in range(HALVES)
+            ]
+            nc.vector.tensor_tensor(
+                out=woven[:].rearrange("p (s u i) -> p s u i", u=HALVES, i=2), in0=halves[0], in1=halves[1], op=ADD
+            )
+            return woven
+
+        def project(woven, t0, t1):
+            width = t1 - t0
             ccodes = cpool.tile([P, width], U32, align_bytes=64, name="ccodes")
             cscales = cpool.tile([P, width], U8, align_bytes=64, name="cscales")
-            nc.vector.quantize_mx(
-                out=ccodes[:].bitcast(FP8X4), scales=cscales[:], in_=gated[gi][:].rearrange("p s r -> p (s r)")
-            )
-            ccodes_of[gi] = ccodes, cscales
-
-        def PM(gi):
-            width = GROUPS[gi][1] * C
-            ccodes, cscales = ccodes_of.pop(gi)
-            o = opsum.tile([P, 4, 2 * C], F32, name="o")
-            for f in range(M // P):
+            nc.vector.quantize_mx(out=ccodes[:].bitcast(FP8X4), scales=cscales[:], in_=woven[:])
+            banks = [opsum.tile([P, 2, width], F32, name="oa"), opsum.tile([P, 1, width], F32, name="ob")]
+            staged = opool.tile([P, F_BLOCKS, width], F32, name="staged")
+            for f in range(F_BLOCKS):
                 nc.tensor.matmul_mx(
-                    out=o[:, f, 0:width],
+                    out=banks[f // 2][:, f % 2, :],
                     lhsT=wpcodes[:, f * P:(f + 1) * P].bitcast(FP8X4),
                     lhsT_scale=wpscales[:, f * P:(f + 1) * P],
                     rhs=ccodes[:].bitcast(FP8X4),
@@ -211,155 +198,43 @@ def tile_moe_nxt_lin_none_kernel(tc, xT, w, wp, gate, offs, out):
                     start=True,
                     stop=True,
                 )
-            projected[gi] = o
+            copy("s", staged[:, 0:2, :], banks[0][:])
+            copy("v" if t1 == T else "s", staged[:, 2:3, :], banks[1][:])
+            nc.sync.dma_start(out[:, t0:t1].rearrange("(f p) t -> p f t", p=P), staged[:])
 
-        def EV(gi, f):
-            first, size = GROUPS[gi]
-            s0, s1 = first * C, (first + size) * C
-            copy(LAST_ENGINE[gi * 3 + f], oslots[f][:, s0:s1], projected[gi][:, f, 0:s1 - s0])
+        for a, t0, t1, engine in X_CHUNKS:
+            quantize_x(load_x(a, t0, t1), a, t0, t1, engine)
+            if a == 0 and t1 == T:
+                for s0, s1 in GATHERS:
+                    gather_codes(0, s0, s1)
+        for s0, s1 in GATHERS:
+            gather_codes(1, s0, s1)
+            gather_scales(s0, s1)
 
-        def SC(i, f):
-            a0, a1 = CUTS[i]
-            nc.vector.tensor_copy(
-                out=windows[f][:].indirect(offsets[:, a0 // 16:a1 // 16]), in_=oslots[f][:, a0:a1]
-            )
+        def finish(e, quantized):
+            expert(e, quantized)
+            for s0, s1 in CUTS:
+                if e * C < s1 <= (e + 1) * C:
+                    scatter(s0, s1)
 
-        def ST(f):
-            nc.sync.dma_start(out[f * P:(f + 1) * P, :], windows[f][:])
+        quantized = [quantize_w(a, load_w(a)) for a in range(PASSES)]
+        for e in range(1, E):
+            raws = [load_w(e * PASSES + a) for a in range(PASSES)]
+            if e < E - 1:
+                load_gates(e - 1, e)
+                first = quantize_w(e * PASSES, raws[0])
+                finish(e - 1, quantized)
+                quantized = [first, quantize_w(e * PASSES + 1, raws[1])]
+            else:
+                nc.sync.dma_start(wpraw[:], wp.rearrange("(q r) f -> q r f", r=PACK))
+                load_gates(e - 1, E)
+                last = [quantize_w(e * PASSES + a, raws[a]) for a in range(PASSES)]
+                finish(e - 1, quantized)
+                finish(e, last)
 
-        LX(0)
-        GX(0)
-        QX(0)
-        LX(2)
-        GX(2)
-        QX(2)
-        LX(1)
-        GX(1)
-        QX(1)
-        GA(0, 0)
-        GA(0, 1)
-        LX(4)
-        GX(4)
-        QX(4)
-        LX(3)
-        GX(3)
-        QX(3)
-        LW(0)
-        GW(0)
-        LX(5)
-        GX(5)
-        QX(5)
-        GA(1, 0)
-        GA(1, 1)
-        LW(1)
-        LG()
-        LP()
-        LW(2)
-        LW(3)
-        LW(4)
-        GS(0)
-        GS(1)
-        GW(1)
-        QW(0)
-        QW(1)
-        GW(2)
-        GW(3)
-        LW(5)
-        GP()
-        QP(0)
-        QP(1)
-        MM(0)
-        GT(0)
-        QW(2)
-        QW(3)
-        GW(4)
-        LW(6)
-        GW(5)
-        LW(7)
-        MM(1)
-        GT(1)
-        QW(4)
-        QW(5)
-        QC(0)
-        PM(0)
-        EV(0, 0)
-        EV(0, 1)
-        EV(0, 2)
-        GW(6)
-        LW(8)
-        GW(7)
-        LW(9)
-        MM(2)
-        GT(2)
-        QW(6)
-        QW(7)
-        GW(8)
-        LW(10)
-        GW(9)
-        LW(11)
-        MM(3)
-        GT(3)
-        QW(8)
-        QW(9)
-        QC(1)
-        PM(1)
-        EV(1, 0)
-        EV(1, 1)
-        EV(1, 2)
-        GW(10)
-        LW(12)
-        GW(11)
-        LW(13)
-        MM(4)
-        GT(4)
-        QW(10)
-        QW(11)
-        SC(0, 0)
-        SC(0, 1)
-        SC(0, 2)
-        GW(12)
-        LW(14)
-        GW(13)
-        LW(15)
-        MM(5)
-        GT(5)
-        QW(12)
-        QW(13)
-        QC(2)
-        PM(2)
-        EV(2, 0)
-        EV(2, 1)
-        EV(2, 2)
-        GW(14)
-        GW(15)
-        MM(6)
-        GT(6)
-        QW(14)
-        QW(15)
-        QC(3)
-        PM(3)
-        EV(3, 0)
-        EV(3, 1)
-        EV(3, 2)
-        MM(7)
-        GT(7)
-        QC(4)
-        PM(4)
-        EV(4, 0)
-        EV(4, 1)
-        EV(4, 2)
-        SC(1, 0)
-        SC(1, 1)
-        SC(1, 2)
-        SC(2, 0)
-        SC(2, 1)
-        SC(2, 2)
-        SC(3, 0)
-        SC(3, 1)
-        SC(3, 2)
-        SC(4, 0)
-        SC(4, 1)
-        SC(4, 2)
-        ST(0)
-        ST(1)
-        ST(2)
+        quantize_wp()
+        woven = weave(*TOKEN_CHUNKS[0])
+        for i, (t0, t1) in enumerate(TOKEN_CHUNKS):
+            ahead = weave(*TOKEN_CHUNKS[i + 1]) if i + 1 < len(TOKEN_CHUNKS) else None
+            project(woven, t0, t1)
+            woven = ahead

@@ -16,7 +16,6 @@ U8 = mybir.dt.uint8
 FP8X4 = mybir.dt.float8_e4m3fn_x4
 ADD = mybir.AluOpType.add
 MULT = mybir.AluOpType.mult
-COPY = mybir.ActivationFunctionType.Copy
 
 P = 128
 PACK = 4
@@ -27,7 +26,7 @@ F_BLOCKS = M // P
 X_CHUNKS = ((0, 0, 512, "s"), (0, 512, 1024, "v"), (0, 1024, 1280, "s"), (1, 0, 512, "s"), (1, 512, 1024, "v"), (1, 1024, 1280, "s"))
 GATHERS = ((0, 256), (256, 640), (640, 1024))
 CUTS = ((0, 192), (192, 384), (384, 576), (576, 768), (768, 1024))
-VECTOR_SHARE = (0, 0, 0, 0, 0, 0, 0, 0, 0, 0, 0, 0, 0, 0, 0, 64)
+VECTOR_SHARE = (0, 0, 0, 0, 0, 0, 0, 0, 0, 0, 0, 0, 0, 0, 0, 2)
 BLOCK = 256
 ZEROS = T // BLOCK
 TOKEN_CHUNKS = ((0, 256), (256, 512), (512, 768), (768, 1024), (1024, 1152), (1152, 1280))
@@ -70,7 +69,7 @@ def tile_moe_nxt_lin_none_kernel(tc, xT, w, wp, gate, offs, out):
             if engine == "v":
                 nc.vector.tensor_copy(out=dst, in_=src)
             else:
-                nc.scalar.activation(out=dst, in_=src, func=COPY)
+                nc.scalar.copy(out=dst, in_=src)
 
         def offsets_of(s0, s1):
             return offsets[:, s0 // 16:s1 // 16]
@@ -105,12 +104,12 @@ def tile_moe_nxt_lin_none_kernel(tc, xT, w, wp, gate, offs, out):
 
         def quantize_w(k, raw):
             grouped = wbf.tile([P, N * PACK], BF16, align_bytes=64, name="grouped")
-            dst = grouped[:].rearrange("p (t m j) -> p m j t", t=PACK, j=PACK)
-            src = raw[:].rearrange("p j (m t) -> p m j t", t=PACK)
-            split = P - VECTOR_SHARE[k]
-            copy("s", dst[:, 0:split], src[:, 0:split])
-            if split < P:
-                copy("v", dst[:, split:P], src[:, split:P])
+            dst = grouped[:].rearrange("p (t c i j) -> p t c j i", t=PACK, i=4, j=PACK)
+            src = raw[:].rearrange("p j (c t i) -> p t c j i", t=PACK, i=4)
+            split = VECTOR_SHARE[k]
+            if split:
+                copy("v", dst[:, 0:split], src[:, 0:split])
+            copy("s", dst[:, split:PACK], src[:, split:PACK])
             codes = wq.tile([P, N], U32, align_bytes=64, name="codes")
             scales = wq.tile([P, N], U8, align_bytes=64, name="scales")
             nc.vector.quantize_mx(out=codes[:].bitcast(FP8X4), scales=scales[:], in_=grouped[:])
@@ -226,7 +225,9 @@ def tile_moe_nxt_lin_none_kernel(tc, xT, w, wp, gate, offs, out):
                 finish(e - 1, quantized)
                 quantized = [first, quantize_w(e * PASSES + 1, raws[1])]
             else:
-                nc.sync.dma_start(wpraw[:], wp.rearrange("(q r) f -> q r f", r=PACK))
+                rows = wp.rearrange("(c t i) f -> i c t f", t=PACK, i=4)
+                for i in range(4):
+                    nc.sync.dma_start(wpraw[i:P:4, :, :], rows[i])
                 load_gates(e - 1, E)
                 last = [quantize_w(e * PASSES + a, raws[a]) for a in range(PASSES)]
                 finish(e - 1, quantized)

@@ -26,10 +26,11 @@ F_BLOCKS = M // P
 X_CHUNKS = ((0, 0, 512, "s"), (0, 512, 1024, "v"), (0, 1024, 1280, "s"), (1, 0, 512, "s"), (1, 512, 1024, "v"), (1, 1024, 1280, "s"))
 GATHERS = ((0, 256), (256, 640), (640, 1024))
 CUTS = ((0, 192), (192, 384), (384, 576), (576, 768), (768, 1024))
-VECTOR_SHARE = (0, 0, 0, 0, 0, 0, 0, 0, 0, 0, 0, 0, 0, 0, 0, 2)
+VECTOR_SHARE = (0, 0, 1, 0, 1, 0, 1, 0, 1, 0, 1, 0, 1, 0, 0, 2)
+BANK = 512
 BLOCK = 256
 ZEROS = T // BLOCK
-TOKEN_CHUNKS = ((0, 256), (256, 512), (512, 768), (768, 1024), (1024, 1152), (1152, 1280))
+TOKEN_CHUNKS = ((0, 256), (256, 512), (512, 768), (768, 1280))
 
 
 def tile_moe_nxt_lin_none_kernel(tc, xT, w, wp, gate, offs, out):
@@ -44,7 +45,7 @@ def tile_moe_nxt_lin_none_kernel(tc, xT, w, wp, gate, offs, out):
         cpool = ctx.enter_context(tc.tile_pool(name="c", bufs=3))
         opool = ctx.enter_context(tc.tile_pool(name="o", bufs=len(TOKEN_CHUNKS)))
         ypsum = ctx.enter_context(tc.psum_pool(name="ypsum", bufs=2))
-        opsum = ctx.enter_context(tc.psum_pool(name="opsum", bufs=2))
+        opsum = ctx.enter_context(tc.psum_pool(name="opsum", bufs=4))
 
         offsets = keep.tile([P, SLOTS // 16], U16, name="offsets")
         nc.sync.dma_start(offsets[:], offs)
@@ -112,7 +113,13 @@ def tile_moe_nxt_lin_none_kernel(tc, xT, w, wp, gate, offs, out):
             copy("s", dst[:, split:PACK], src[:, split:PACK])
             codes = wq.tile([P, N], U32, align_bytes=64, name="codes")
             scales = wq.tile([P, N], U8, align_bytes=64, name="scales")
-            nc.vector.quantize_mx(out=codes[:].bitcast(FP8X4), scales=scales[:], in_=grouped[:])
+            width = N // HALVES if k == E * PASSES - 1 else N
+            for n0 in range(0, N, width):
+                nc.vector.quantize_mx(
+                    out=codes[:, n0:n0 + width].bitcast(FP8X4),
+                    scales=scales[:, n0:n0 + width],
+                    in_=grouped[:, n0 * PACK:(n0 + width) * PACK],
+                )
             return codes, scales
 
         def expert(e, quantized):
@@ -185,21 +192,33 @@ def tile_moe_nxt_lin_none_kernel(tc, xT, w, wp, gate, offs, out):
             ccodes = cpool.tile([P, width], U32, align_bytes=64, name="ccodes")
             cscales = cpool.tile([P, width], U8, align_bytes=64, name="cscales")
             nc.vector.quantize_mx(out=ccodes[:].bitcast(FP8X4), scales=cscales[:], in_=woven[:])
-            banks = [opsum.tile([P, 2, width], F32, name="oa"), opsum.tile([P, 1, width], F32, name="ob")]
             staged = opool.tile([P, F_BLOCKS, width], F32, name="staged")
-            for f in range(F_BLOCKS):
-                nc.tensor.matmul_mx(
-                    out=banks[f // 2][:, f % 2, :],
-                    lhsT=wpcodes[:, f * P:(f + 1) * P].bitcast(FP8X4),
-                    lhsT_scale=wpscales[:, f * P:(f + 1) * P],
-                    rhs=ccodes[:].bitcast(FP8X4),
-                    rhs_scale=cscales[:],
-                    start=True,
-                    stop=True,
-                )
-            copy("s", staged[:, 0:2, :], banks[0][:])
-            copy("v" if t1 == T else "s", staged[:, 2:3, :], banks[1][:])
-            nc.sync.dma_start(out[:, t0:t1].rearrange("(f p) t -> p f t", p=P), staged[:])
+            rows = out[:, t0:t1].rearrange("(f p) t -> p f t", p=P)
+            for f0 in range(0, F_BLOCKS, BANK // width):
+                f1 = min(f0 + BANK // width, F_BLOCKS)
+                bank = opsum.tile([P, f1 - f0, width], F32, name="bank")
+                for f in range(f0, f1):
+                    nc.tensor.matmul_mx(
+                        out=bank[:, f - f0, :],
+                        lhsT=wpcodes[:, f * P:(f + 1) * P].bitcast(FP8X4),
+                        lhsT_scale=wpscales[:, f * P:(f + 1) * P],
+                        rhs=ccodes[:].bitcast(FP8X4),
+                        rhs_scale=cscales[:],
+                        start=True,
+                        stop=True,
+                    )
+                copy("v" if width == BANK and f0 == 1 else "s", staged[:, f0:f1, :], bank[:])
+                if width == BANK:
+                    nc.sync.dma_start(rows[:, f0:f1, :], staged[:, f0:f1, :])
+            if width < BANK:
+                nc.sync.dma_start(rows, staged[:])
+
+        def weave_on_scalar(t0, t1):
+            woven = keep.tile([P, (t1 - t0) * PACK], BF16, align_bytes=64, name="woven_last")
+            words = woven[:].bitcast(F32).rearrange("p (s u) -> p s u", u=HALVES)
+            for u in range(HALVES):
+                nc.scalar.copy(out=words[:, :, u], in_=windows[u][:, t0:t1])
+            return woven
 
         for a, t0, t1, engine in X_CHUNKS:
             quantize_x(load_x(a, t0, t1), a, t0, t1, engine)
@@ -225,17 +244,16 @@ def tile_moe_nxt_lin_none_kernel(tc, xT, w, wp, gate, offs, out):
                 finish(e - 1, quantized)
                 quantized = [first, quantize_w(e * PASSES + 1, raws[1])]
             else:
-                rows = wp.rearrange("(c t i) f -> i c t f", t=PACK, i=4)
-                for i in range(4):
-                    nc.sync.dma_start(wpraw[i:P:4, :, :], rows[i])
+                rows = wp.rearrange("(c t i) f -> t c i f", t=PACK, i=4)
+                for t in range(PACK):
+                    nc.sync.dma_start(wpraw[:, t, :], rows[t])
                 load_gates(e - 1, E)
                 last = [quantize_w(e * PASSES + a, raws[a]) for a in range(PASSES)]
                 finish(e - 1, quantized)
                 finish(e, last)
 
         quantize_wp()
-        woven = weave(*TOKEN_CHUNKS[0])
-        for i, (t0, t1) in enumerate(TOKEN_CHUNKS):
-            ahead = weave(*TOKEN_CHUNKS[i + 1]) if i + 1 < len(TOKEN_CHUNKS) else None
-            project(woven, t0, t1)
-            woven = ahead
+        woven_last = weave_on_scalar(*TOKEN_CHUNKS[-1])
+        for t0, t1 in TOKEN_CHUNKS[:-1]:
+            project(weave(t0, t1), t0, t1)
+        project(woven_last, *TOKEN_CHUNKS[-1])

@@ -23,7 +23,12 @@ KP = P * PACK
 PASSES = K // KP
 HALVES = 2
 F_BLOCKS = M // P
-X_CHUNKS = ((0, 0, 512, "s"), (0, 512, 1024, "v"), (0, 1024, 1280, "s"), (1, 0, 512, "s"), (1, 512, 1024, "v"), (1, 1024, 1280, "s"))
+X_LOADS = (((0, 1280),), ((0, 768), (768, 1280)))
+X_COPIES = (
+    ((0, 512, "v"), (768, 1280, "s"), (512, 768, "v")),
+    ((0, 512, "s"), (512, 768, "s"), (768, 1024, "s"), (1024, 1280, "v")),
+)
+X_QUANTIZE = (((0, 512), (512, 768), (768, 1280)), ((0, 512), (512, 768), (768, 1280)))
 GATHERS = ((0, 256), (256, 640), (640, 1024))
 CUTS = ((0, 192), (192, 384), (384, 576), (576, 768), (768, 1024))
 VECTOR_SHARE = (0, 0, 1, 0, 1, 0, 1, 0, 1, 0, 1, 0, 1, 0, 0, 2)
@@ -37,8 +42,7 @@ def tile_moe_nxt_lin_none_kernel(tc, xT, w, wp, gate, offs, out):
     nc = tc.nc
     with ExitStack() as ctx:
         keep = ctx.enter_context(tc.tile_pool(name="keep", bufs=1))
-        xraw = ctx.enter_context(tc.tile_pool(name="xraw", bufs=6))
-        xbf = ctx.enter_context(tc.tile_pool(name="xbf", bufs=3))
+        xbf = ctx.enter_context(tc.tile_pool(name="xbf", bufs=PASSES))
         wraw = ctx.enter_context(tc.tile_pool(name="wraw", bufs=6))
         wbf = ctx.enter_context(tc.tile_pool(name="wbf", bufs=4))
         wq = ctx.enter_context(tc.tile_pool(name="wq", bufs=5))
@@ -48,8 +52,6 @@ def tile_moe_nxt_lin_none_kernel(tc, xT, w, wp, gate, offs, out):
         opsum = ctx.enter_context(tc.psum_pool(name="opsum", bufs=4))
 
         offsets = keep.tile([P, SLOTS // 16], U16, name="offsets")
-        nc.sync.dma_start(offsets[:], offs)
-
         xcodes = [keep.tile([P, T], U32, align_bytes=64, name="xcodes%d" % a) for a in range(PASSES)]
         xscales = keep.tile([P, T], U8, align_bytes=64, name="xscales")
         gcodes = [keep.tile([P, SLOTS], U32, align_bytes=64, name="gcodes%d" % a) for a in range(PASSES)]
@@ -75,21 +77,27 @@ def tile_moe_nxt_lin_none_kernel(tc, xT, w, wp, gate, offs, out):
         def offsets_of(s0, s1):
             return offsets[:, s0 // 16:s1 // 16]
 
-        def load_x(a, t0, t1):
-            xr = xraw.tile([P, PACK, t1 - t0], F32, name="xr")
-            nc.sync.dma_start(xr[:], xT[a * KP:(a + 1) * KP, t0:t1].rearrange("(p j) t -> p j t", j=PACK))
-            return xr
-
-        def quantize_x(xr, a, t0, t1, engine):
-            xb = xbf.tile([P, (t1 - t0) * PACK], BF16, align_bytes=64, name="xb")
-            copy(
-                engine,
-                xb[:].rearrange("p (c i j) -> p c j i", i=4, j=PACK),
-                xr[:].rearrange("p j (c i) -> p c j i", i=4),
-            )
-            nc.vector.quantize_mx(
-                out=xcodes[a][:, t0:t1].bitcast(FP8X4), scales=xscales[PACK * a:P, t0:t1], in_=xb[:]
-            )
+        def quantize_x(a):
+            xb = xbf.tile([P, T * PACK], BF16, align_bytes=64, name="xb")
+            for l0, l1 in X_LOADS[a]:
+                xr = keep.tile([P, PACK, l1 - l0], F32, name="xr%d_%d" % (a, l0))
+                nc.sync.dma_start(xr[:], xT[a * KP:(a + 1) * KP, l0:l1].rearrange("(p j) t -> p j t", j=PACK))
+                if a == 0 and l0 == 0:
+                    nc.sync.dma_start(offsets[:], offs)
+                for t0, t1, engine in X_COPIES[a]:
+                    if l0 <= t0 < l1:
+                        copy(
+                            engine,
+                            xb[:, t0 * PACK:t1 * PACK].rearrange("p (c i j) -> p c j i", i=4, j=PACK),
+                            xr[:, :, t0 - l0:t1 - l0].rearrange("p j (c i) -> p c j i", i=4),
+                        )
+                for q0, q1 in X_QUANTIZE[a]:
+                    if l0 < q1 <= l1:
+                        nc.vector.quantize_mx(
+                            out=xcodes[a][:, q0:q1].bitcast(FP8X4),
+                            scales=xscales[PACK * a:P, q0:q1],
+                            in_=xb[:, q0 * PACK:q1 * PACK],
+                        )
 
         def gather_codes(a, s0, s1):
             nc.vector.tensor_copy(out=gcodes[a][:, s0:s1], in_=xcodes[a][:].indirect(offsets_of(s0, s1)))
@@ -220,11 +228,10 @@ def tile_moe_nxt_lin_none_kernel(tc, xT, w, wp, gate, offs, out):
                 nc.scalar.copy(out=words[:, :, u], in_=windows[u][:, t0:t1])
             return woven
 
-        for a, t0, t1, engine in X_CHUNKS:
-            quantize_x(load_x(a, t0, t1), a, t0, t1, engine)
-            if a == 0 and t1 == T:
-                for s0, s1 in GATHERS:
-                    gather_codes(0, s0, s1)
+        quantize_x(0)
+        for s0, s1 in GATHERS:
+            gather_codes(0, s0, s1)
+        quantize_x(1)
         for s0, s1 in GATHERS:
             gather_codes(1, s0, s1)
             gather_scales(s0, s1)

@@ -29,9 +29,9 @@ X_COPIES = (
     ((0, 512, "s"), (512, 768, "s"), (768, 1024, "s"), (1024, 1280, "v")),
 )
 X_QUANTIZE = (((0, 512), (512, 768), (768, 1280)), ((0, 512), (512, 768), (768, 1280)))
-GATHERS = ((0, 256), (256, 640), (640, 1024))
+GATHERS = ((0, 512), (512, 1024))
 CUTS = ((0, 192), (192, 384), (384, 576), (576, 768), (768, 1024))
-VECTOR_SHARE = (0, 0, 1, 0, 1, 0, 1, 0, 1, 0, 1, 0, 1, 0, 0, 2)
+VECTOR_SHARE = (0, 0, 0, 1, 0, 0, 0, 0, 0, 2, 0, 0, 0, 0, 0, 2)
 BANK = 512
 BLOCK = 256
 ZEROS = T // BLOCK

@@ -1,6 +1,7 @@
 from contextlib import ExitStack
 
 import concourse.mybir as mybir
+from concourse.masks import make_identity
 
 K, T, E, C, N, M = 1024, 1280, 8, 128, 512, 384
 SLOTS = E * C
@@ -23,15 +24,15 @@ KP = P * PACK
 PASSES = K // KP
 HALVES = 2
 F_BLOCKS = M // P
-X_LOADS = (((0, 1280),), ((0, 768), (768, 1280)))
+X_LOADS = (((0, 512), (512, 1280)), ((0, 768), (768, 1280)))
 X_COPIES = (
-    ((0, 512, "v"), (768, 1280, "s"), (512, 768, "v")),
-    ((0, 512, "s"), (512, 768, "s"), (768, 1024, "s"), (1024, 1280, "v")),
+    ((0, 512, "v"), (512, 768, "s"), (768, 1280, "v")),
+    ((0, 512, "s"), (512, 768, "v"), (768, 1024, "s"), (1024, 1280, "v")),
 )
-X_QUANTIZE = (((0, 512), (512, 768), (768, 1280)), ((0, 512), (512, 768), (768, 1280)))
+X_QUANTIZE = (((0, 512), (768, 1280), (512, 768)), ((512, 768), (0, 512), (768, 1280)))
 GATHERS = ((0, 512), (512, 1024))
-CUTS = ((0, 192), (192, 384), (384, 576), (576, 768), (768, 1024))
-VECTOR_SHARE = (0, 0, 0, 1, 0, 0, 0, 0, 0, 2, 0, 0, 0, 0, 0, 2)
+CUTS = ((0, 256), (256, 512), (512, 768), (768, 1024))
+VECTOR_SHARE = (0, 0, 1, 0, 1, 0, 1, 0, 1, 0, 1, 0, 1, 0, 0, 2)
 BANK = 512
 BLOCK = 256
 ZEROS = T // BLOCK
@@ -57,6 +58,10 @@ def tile_moe_nxt_lin_none_kernel(tc, xT, w, wp, gate, offs, out):
         gcodes = [keep.tile([P, SLOTS], U32, align_bytes=64, name="gcodes%d" % a) for a in range(PASSES)]
         gscales = keep.tile([P, SLOTS], U8, align_bytes=64, name="gscales")
         gates = {}
+        identity = keep.tile([P, P], F32, name="identity")
+        gate_rows = keep.tile([P, C], F32, name="gate_rows")
+        gate_columns = keep.tile([P, E // 2], F32, name="gate_columns")
+        spread = keep.tile([P, E // 2, C], F32, name="spread")
         wpraw = keep.tile([P, PACK, M], F32, name="wpraw")
         wpbf = keep.tile([P, M, PACK], BF16, align_bytes=64, name="wpbf")
         wpcodes = keep.tile([P, M], U32, align_bytes=64, name="wpcodes")
@@ -160,6 +165,19 @@ def tile_moe_nxt_lin_none_kernel(tc, xT, w, wp, gate, offs, out):
             for e in range(e0, e1):
                 gates[e] = tile[:, (e - e0) * C:(e - e0 + 1) * C]
 
+        def spread_odd_gates():
+            make_identity(nc, identity[:])
+            nc.gpsimd.memset(gate_rows[:], 0.0)
+            nc.sync.dma_start(gate_rows[0:E // 2, :], gate[0, :].rearrange("(h o s) -> o h s", o=2, s=C)[1])
+            turned = opsum.tile([P, P], F32, name="bank")
+            nc.tensor.transpose(turned[:], gate_rows[:], identity[:])
+            nc.scalar.copy(out=gate_columns[:], in_=turned[:, 0:E // 2])
+            bank = opsum.tile([P, E // 2, C], F32, name="bank")
+            for h in range(E // 2):
+                nc.tensor.transpose(bank[:, h, :], gate_columns[:, h:h + 1].to_broadcast([P, P]), identity[:])
+                gates[2 * h + 1] = spread[:, h, :]
+            nc.scalar.copy(out=spread[:], in_=bank[:])
+
         def scatter(s0, s1):
             for u in range(HALVES):
                 nc.vector.tensor_copy(
@@ -228,6 +246,7 @@ def tile_moe_nxt_lin_none_kernel(tc, xT, w, wp, gate, offs, out):
                 nc.scalar.copy(out=words[:, :, u], in_=windows[u][:, t0:t1])
             return woven
 
+        spread_odd_gates()
         quantize_x(0)
         for s0, s1 in GATHERS:
             gather_codes(0, s0, s1)
@@ -246,7 +265,8 @@ def tile_moe_nxt_lin_none_kernel(tc, xT, w, wp, gate, offs, out):
         for e in range(1, E):
             raws = [load_w(e * PASSES + a) for a in range(PASSES)]
             if e < E - 1:
-                load_gates(e - 1, e)
+                if e % 2:
+                    load_gates(e - 1, e)
                 first = quantize_w(e * PASSES, raws[0])
                 finish(e - 1, quantized)
                 quantized = [first, quantize_w(e * PASSES + 1, raws[1])]
@@ -254,7 +274,7 @@ def tile_moe_nxt_lin_none_kernel(tc, xT, w, wp, gate, offs, out):
                 rows = wp.rearrange("(c t i) f -> t c i f", t=PACK, i=4)
                 for t in range(PACK):
                     nc.sync.dma_start(wpraw[:, t, :], rows[t])
-                load_gates(e - 1, E)
+                load_gates(e - 1, e)
                 last = [quantize_w(e * PASSES + a, raws[a]) for a in range(PASSES)]
                 finish(e - 1, quantized)
                 finish(e, last)

@@ -33,6 +33,7 @@ X_QUANTIZE = (((0, 512), (768, 1280), (512, 768)), ((512, 768), (0, 512), (768, 
 GATHERS = ((0, 512), (512, 1024))
 CUTS = ((0, 256), (256, 512), (512, 768), (768, 1024))
 VECTOR_SHARE = (0, 0, 1, 0, 1, 0, 1, 0, 1, 0, 1, 0, 1, 0, 0, 2)
+SPREAD = E - 2
 BANK = 512
 BLOCK = 256
 ZEROS = T // BLOCK
@@ -60,8 +61,8 @@ def tile_moe_nxt_lin_none_kernel(tc, xT, w, wp, gate, offs, out):
         gates = {}
         identity = keep.tile([P, P], F32, name="identity")
         gate_rows = keep.tile([P, C], F32, name="gate_rows")
-        gate_columns = keep.tile([P, E // 2], F32, name="gate_columns")
-        spread = keep.tile([P, E // 2, C], F32, name="spread")
+        gate_columns = keep.tile([P, SPREAD], F32, name="gate_columns")
+        spread = keep.tile([P, SPREAD, C], F32, name="spread")
         wpraw = keep.tile([P, PACK, M], F32, name="wpraw")
         wpbf = keep.tile([P, M, PACK], BF16, align_bytes=64, name="wpbf")
         wpcodes = keep.tile([P, M], U32, align_bytes=64, name="wpcodes")
@@ -126,7 +127,7 @@ def tile_moe_nxt_lin_none_kernel(tc, xT, w, wp, gate, offs, out):
             copy("s", dst[:, split:PACK], src[:, split:PACK])
             codes = wq.tile([P, N], U32, align_bytes=64, name="codes")
             scales = wq.tile([P, N], U8, align_bytes=64, name="scales")
-            width = N // HALVES if k == E * PASSES - 1 else N
+            width = N // HALVES if k % PASSES == PASSES - 1 and k != 2 * (E - 2) + 1 else N
             for n0 in range(0, N, width):
                 nc.vector.quantize_mx(
                     out=codes[:, n0:n0 + width].bitcast(FP8X4),
@@ -165,18 +166,19 @@ def tile_moe_nxt_lin_none_kernel(tc, xT, w, wp, gate, offs, out):
             for e in range(e0, e1):
                 gates[e] = tile[:, (e - e0) * C:(e - e0 + 1) * C]
 
-        def spread_odd_gates():
+        def spread_gates():
             make_identity(nc, identity[:])
             nc.gpsimd.memset(gate_rows[:], 0.0)
-            nc.sync.dma_start(gate_rows[0:E // 2, :], gate[0, :].rearrange("(h o s) -> o h s", o=2, s=C)[1])
+            nc.sync.dma_start(gate_rows[0:SPREAD, :], gate[0, 0:SPREAD * C].rearrange("(e s) -> e s", s=C))
             turned = opsum.tile([P, P], F32, name="bank")
             nc.tensor.transpose(turned[:], gate_rows[:], identity[:])
-            nc.scalar.copy(out=gate_columns[:], in_=turned[:, 0:E // 2])
-            bank = opsum.tile([P, E // 2, C], F32, name="bank")
-            for h in range(E // 2):
-                nc.tensor.transpose(bank[:, h, :], gate_columns[:, h:h + 1].to_broadcast([P, P]), identity[:])
-                gates[2 * h + 1] = spread[:, h, :]
-            nc.scalar.copy(out=spread[:], in_=bank[:])
+            nc.scalar.copy(out=gate_columns[:], in_=turned[:, 0:SPREAD])
+            for e0 in range(0, SPREAD, SPREAD // 2):
+                bank = opsum.tile([P, SPREAD // 2, C], F32, name="bank")
+                for e in range(e0, e0 + SPREAD // 2):
+                    nc.tensor.transpose(bank[:, e - e0, :], gate_columns[:, e:e + 1].to_broadcast([P, P]), identity[:])
+                    gates[e] = spread[:, e, :]
+                nc.scalar.copy(out=spread[:, e0:e0 + SPREAD // 2, :], in_=bank[:])
 
         def scatter(s0, s1):
             for u in range(HALVES):
@@ -246,7 +248,7 @@ def tile_moe_nxt_lin_none_kernel(tc, xT, w, wp, gate, offs, out):
                 nc.scalar.copy(out=words[:, :, u], in_=windows[u][:, t0:t1])
             return woven
 
-        spread_odd_gates()
+        spread_gates()
         quantize_x(0)
         for s0, s1 in GATHERS:
             gather_codes(0, s0, s1)
@@ -265,8 +267,6 @@ def tile_moe_nxt_lin_none_kernel(tc, xT, w, wp, gate, offs, out):
         for e in range(1, E):
             raws = [load_w(e * PASSES + a) for a in range(PASSES)]
             if e < E - 1:
-                if e % 2:
-                    load_gates(e - 1, e)
                 first = quantize_w(e * PASSES, raws[0])
                 finish(e - 1, quantized)
                 quantized = [first, quantize_w(e * PASSES + 1, raws[1])]
@@ -274,7 +274,7 @@ def tile_moe_nxt_lin_none_kernel(tc, xT, w, wp, gate, offs, out):
                 rows = wp.rearrange("(c t i) f -> t c i f", t=PACK, i=4)
                 for t in range(PACK):
                     nc.sync.dma_start(wpraw[:, t, :], rows[t])
-                load_gates(e - 1, e)
+                load_gates(e - 1, E)
                 last = [quantize_w(e * PASSES + a, raws[a]) for a in range(PASSES)]
                 finish(e - 1, quantized)
                 finish(e, last)

@@ -24,16 +24,12 @@ KP = P * PACK
 PASSES = K // KP
 HALVES = 2
 F_BLOCKS = M // P
-X_LOADS = (((0, 512), (512, 1280)), ((0, 768), (768, 1280)))
-X_COPIES = (
-    ((0, 512, "v"), (512, 768, "s"), (768, 1280, "v")),
-    ((0, 512, "s"), (512, 768, "v"), (768, 1024, "s"), (1024, 1280, "v")),
-)
-X_QUANTIZE = (((0, 512), (768, 1280), (512, 768)), ((512, 768), (0, 512), (768, 1280)))
+X_COPIES = ((0, 512, "v"), (768, 1280, "s"), (512, 768, "v"))
+X_QUANTIZE = ((0, 512), (512, 768), (768, 1280))
 GATHERS = ((0, 512), (512, 1024))
-CUTS = ((0, 256), (256, 512), (512, 768), (768, 1024))
-VECTOR_SHARE = (0, 0, 1, 0, 1, 0, 1, 0, 1, 0, 1, 0, 1, 0, 0, 2)
-SPREAD = E - 2
+TWINS = 2
+LAST = TWINS * PASSES - 1
+VECTOR_SHARE = 2
 BANK = 512
 BLOCK = 256
 ZEROS = T // BLOCK
@@ -45,11 +41,10 @@ def tile_moe_nxt_lin_none_kernel(tc, xT, w, wp, gate, offs, out):
     with ExitStack() as ctx:
         keep = ctx.enter_context(tc.tile_pool(name="keep", bufs=1))
         xbf = ctx.enter_context(tc.tile_pool(name="xbf", bufs=PASSES))
-        wraw = ctx.enter_context(tc.tile_pool(name="wraw", bufs=6))
+        wraw = ctx.enter_context(tc.tile_pool(name="wraw", bufs=4))
         wbf = ctx.enter_context(tc.tile_pool(name="wbf", bufs=4))
-        wq = ctx.enter_context(tc.tile_pool(name="wq", bufs=5))
+        wq = ctx.enter_context(tc.tile_pool(name="wq", bufs=6))
         cpool = ctx.enter_context(tc.tile_pool(name="c", bufs=3))
-        opool = ctx.enter_context(tc.tile_pool(name="o", bufs=len(TOKEN_CHUNKS)))
         ypsum = ctx.enter_context(tc.psum_pool(name="ypsum", bufs=2))
         opsum = ctx.enter_context(tc.psum_pool(name="opsum", bufs=4))
 
@@ -58,16 +53,14 @@ def tile_moe_nxt_lin_none_kernel(tc, xT, w, wp, gate, offs, out):
         xscales = keep.tile([P, T], U8, align_bytes=64, name="xscales")
         gcodes = [keep.tile([P, SLOTS], U32, align_bytes=64, name="gcodes%d" % a) for a in range(PASSES)]
         gscales = keep.tile([P, SLOTS], U8, align_bytes=64, name="gscales")
-        gates = {}
         identity = keep.tile([P, P], F32, name="identity")
         gate_rows = keep.tile([P, C], F32, name="gate_rows")
-        gate_columns = keep.tile([P, SPREAD], F32, name="gate_columns")
-        spread = keep.tile([P, SPREAD, C], F32, name="spread")
+        gate_columns = keep.tile([P, E], F32, name="gate_columns")
+        spread = keep.tile([P, E, C], F32, name="spread")
         wpraw = keep.tile([P, PACK, M], F32, name="wpraw")
         wpbf = keep.tile([P, M, PACK], BF16, align_bytes=64, name="wpbf")
         wpcodes = keep.tile([P, M], U32, align_bytes=64, name="wpcodes")
         wpscales = keep.tile([P, M], U8, align_bytes=64, name="wpscales")
-        pairs = [keep.tile([P, SLOTS * 2], BF16, align_bytes=64, name="pairs%d" % u) for u in range(HALVES)]
         windows = [keep.tile([P, T + BLOCK], F32, name="window%d" % u) for u in range(HALVES)]
 
         nc.vector.memset(xscales[:].bitcast(I32), 0)
@@ -85,25 +78,23 @@ def tile_moe_nxt_lin_none_kernel(tc, xT, w, wp, gate, offs, out):
 
         def quantize_x(a):
             xb = xbf.tile([P, T * PACK], BF16, align_bytes=64, name="xb")
-            for l0, l1 in X_LOADS[a]:
-                xr = keep.tile([P, PACK, l1 - l0], F32, name="xr%d_%d" % (a, l0))
-                nc.sync.dma_start(xr[:], xT[a * KP:(a + 1) * KP, l0:l1].rearrange("(p j) t -> p j t", j=PACK))
-                if a == 0 and l0 == 0:
-                    nc.sync.dma_start(offsets[:], offs)
-                for t0, t1, engine in X_COPIES[a]:
-                    if l0 <= t0 < l1:
-                        copy(
-                            engine,
-                            xb[:, t0 * PACK:t1 * PACK].rearrange("p (c i j) -> p c j i", i=4, j=PACK),
-                            xr[:, :, t0 - l0:t1 - l0].rearrange("p j (c i) -> p c j i", i=4),
-                        )
-                for q0, q1 in X_QUANTIZE[a]:
-                    if l0 < q1 <= l1:
-                        nc.vector.quantize_mx(
-                            out=xcodes[a][:, q0:q1].bitcast(FP8X4),
-                            scales=xscales[PACK * a:P, q0:q1],
-                            in_=xb[:, q0 * PACK:q1 * PACK],
-                        )
+            xr = keep.tile([P, PACK * T], F32, name="xr%d" % a)
+            nc.sync.dma_start(xr[:], xT[a * KP:(a + 1) * KP, :].rearrange("(p j) t -> p (j t)", j=PACK))
+            if a == 0:
+                nc.sync.dma_start(offsets[:], offs)
+            rows = xr[:].rearrange("p (j t) -> p j t", j=PACK)
+            for t0, t1, engine in X_COPIES:
+                copy(
+                    engine,
+                    xb[:, t0 * PACK:t1 * PACK].rearrange("p (c i j) -> p c j i", i=4, j=PACK),
+                    rows[:, :, t0:t1].rearrange("p j (c i) -> p c j i", i=4),
+                )
+            for q0, q1 in X_QUANTIZE:
+                nc.vector.quantize_mx(
+                    out=xcodes[a][:, q0:q1].bitcast(FP8X4),
+                    scales=xscales[PACK * a:P, q0:q1],
+                    in_=xb[:, q0 * PACK:q1 * PACK],
+                )
 
         def gather_codes(a, s0, s1):
             nc.vector.tensor_copy(out=gcodes[a][:, s0:s1], in_=xcodes[a][:].indirect(offsets_of(s0, s1)))
@@ -113,21 +104,24 @@ def tile_moe_nxt_lin_none_kernel(tc, xT, w, wp, gate, offs, out):
 
         def load_w(k):
             e, a = divmod(k, PASSES)
-            raw = wraw.tile([P, PACK, N], F32, name="raw")
-            nc.sync.dma_start(raw[:], w[e, a * KP:(a + 1) * KP, :].rearrange("(p j) n -> p j n", j=PACK))
+            if k % (LAST + 1) == LAST:
+                raw = keep.tile([P, PACK * N], F32, name="raw%d" % k)
+            else:
+                raw = wraw.tile([P, PACK * N], F32, name="raw")
+            nc.sync.dma_start(raw[:], w[e, a * KP:(a + 1) * KP, :].rearrange("(p j) n -> p (j n)", j=PACK))
             return raw
 
         def quantize_w(k, raw):
             grouped = wbf.tile([P, N * PACK], BF16, align_bytes=64, name="grouped")
             dst = grouped[:].rearrange("p (t c i j) -> p t c j i", t=PACK, i=4, j=PACK)
-            src = raw[:].rearrange("p j (c t i) -> p t c j i", t=PACK, i=4)
-            split = VECTOR_SHARE[k]
+            src = raw[:].rearrange("p (j c t i) -> p t c j i", j=PACK, t=PACK, i=4)
+            split = VECTOR_SHARE if k % (LAST + 1) == LAST else 0
             if split:
                 copy("v", dst[:, 0:split], src[:, 0:split])
             copy("s", dst[:, split:PACK], src[:, split:PACK])
             codes = wq.tile([P, N], U32, align_bytes=64, name="codes")
             scales = wq.tile([P, N], U8, align_bytes=64, name="scales")
-            width = N // HALVES if k % PASSES == PASSES - 1 and k != 2 * (E - 2) + 1 else N
+            width = N // HALVES if k % (LAST + 1) == LAST else N
             for n0 in range(0, N, width):
                 nc.vector.quantize_mx(
                     out=codes[:, n0:n0 + width].bitcast(FP8X4),
@@ -136,7 +130,7 @@ def tile_moe_nxt_lin_none_kernel(tc, xT, w, wp, gate, offs, out):
                 )
             return codes, scales
 
-        def expert(e, quantized):
+        def expert(e, quantized, pairs):
             cols = slice(e * C, (e + 1) * C)
             for u in range(HALVES):
                 y = ypsum.tile([P, 2, C], F32, name="y%d" % u)
@@ -154,45 +148,36 @@ def tile_moe_nxt_lin_none_kernel(tc, xT, w, wp, gate, offs, out):
                             stop=(a == PASSES - 1),
                         )
                 nc.vector.tensor_tensor(
-                    out=pairs[u][:, 2 * e * C:2 * (e + 1) * C].rearrange("p (s i) -> p s i", i=2),
+                    out=pairs[u][:, e % TWINS * C:(e % TWINS + 1) * C].bitcast(BF16).rearrange("p (s i) -> p s i", i=2),
                     in0=y[:].rearrange("p i s -> p s i"),
-                    in1=gates[e].unsqueeze(2).to_broadcast([P, C, 2]),
+                    in1=spread[:, e, :].unsqueeze(2).to_broadcast([P, C, 2]),
                     op=MULT,
                 )
-
-        def load_gates(e0, e1):
-            tile = keep.tile([P, (e1 - e0) * C], F32, name="gates%d" % e0)
-            nc.sync.dma_start(tile[:], gate[0:P, e0 * C:e1 * C])
-            for e in range(e0, e1):
-                gates[e] = tile[:, (e - e0) * C:(e - e0 + 1) * C]
 
         def spread_gates():
             make_identity(nc, identity[:])
             nc.gpsimd.memset(gate_rows[:], 0.0)
-            nc.sync.dma_start(gate_rows[0:SPREAD, :], gate[0, 0:SPREAD * C].rearrange("(e s) -> e s", s=C))
+            nc.sync.dma_start(gate_rows[0:E, :], gate[0, :].rearrange("(e s) -> e s", s=C))
             turned = opsum.tile([P, P], F32, name="bank")
             nc.tensor.transpose(turned[:], gate_rows[:], identity[:])
-            nc.scalar.copy(out=gate_columns[:], in_=turned[:, 0:SPREAD])
-            for e0 in range(0, SPREAD, SPREAD // 2):
-                bank = opsum.tile([P, SPREAD // 2, C], F32, name="bank")
-                for e in range(e0, e0 + SPREAD // 2):
+            nc.scalar.copy(out=gate_columns[:], in_=turned[:, 0:E])
+            for e0 in range(0, E, BANK // C):
+                bank = opsum.tile([P, BANK // C, C], F32, name="bank")
+                for e in range(e0, e0 + BANK // C):
                     nc.tensor.transpose(bank[:, e - e0, :], gate_columns[:, e:e + 1].to_broadcast([P, P]), identity[:])
-                    gates[e] = spread[:, e, :]
-                nc.scalar.copy(out=spread[:, e0:e0 + SPREAD // 2, :], in_=bank[:])
+                nc.scalar.copy(out=spread[:, e0:e0 + BANK // C, :], in_=bank[:])
 
-        def scatter(s0, s1):
+        def scatter(s0, s1, pairs):
             for u in range(HALVES):
-                nc.vector.tensor_copy(
-                    out=windows[u][:].indirect(offsets_of(s0, s1)), in_=pairs[u][:, 2 * s0:2 * s1].bitcast(F32)
-                )
+                nc.vector.tensor_copy(out=windows[u][:].indirect(offsets_of(s0, s1)), in_=pairs[u])
 
         def quantize_wp():
-            copy(
-                "s",
-                wpbf[:].rearrange("q (c i) r -> q c r i", i=4),
-                wpraw[:].rearrange("q r (c i) -> q c r i", i=4),
-            )
-            for f0, f1 in ((0, 256), (256, M)):
+            for f0, f1 in ((0, 128), (128, 256), (256, M)):
+                copy(
+                    "s",
+                    wpbf[:, f0:f1, :].rearrange("q (c i) r -> q c r i", i=4),
+                    wpraw[:, :, f0:f1].rearrange("q r (c i) -> q c r i", i=4),
+                )
                 nc.vector.quantize_mx(
                     out=wpcodes[:, f0:f1].bitcast(FP8X4),
                     scales=wpscales[:, f0:f1],
@@ -220,7 +205,7 @@ def tile_moe_nxt_lin_none_kernel(tc, xT, w, wp, gate, offs, out):
             ccodes = cpool.tile([P, width], U32, align_bytes=64, name="ccodes")
             cscales = cpool.tile([P, width], U8, align_bytes=64, name="cscales")
             nc.vector.quantize_mx(out=ccodes[:].bitcast(FP8X4), scales=cscales[:], in_=woven[:])
-            staged = opool.tile([P, F_BLOCKS, width], F32, name="staged")
+            staged = keep.tile([P, F_BLOCKS, width], F32, name="staged%d" % t0)
             rows = out[:, t0:t1].rearrange("(f p) t -> p f t", p=P)
             for f0 in range(0, F_BLOCKS, BANK // width):
                 f1 = min(f0 + BANK // width, F_BLOCKS)
@@ -257,27 +242,18 @@ def tile_moe_nxt_lin_none_kernel(tc, xT, w, wp, gate, offs, out):
             gather_codes(1, s0, s1)
             gather_scales(s0, s1)
 
-        def finish(e, quantized):
-            expert(e, quantized)
-            for s0, s1 in CUTS:
-                if e * C < s1 <= (e + 1) * C:
-                    scatter(s0, s1)
-
-        quantized = [quantize_w(a, load_w(a)) for a in range(PASSES)]
-        for e in range(1, E):
-            raws = [load_w(e * PASSES + a) for a in range(PASSES)]
-            if e < E - 1:
-                first = quantize_w(e * PASSES, raws[0])
-                finish(e - 1, quantized)
-                quantized = [first, quantize_w(e * PASSES + 1, raws[1])]
-            else:
+        for e0 in range(0, E, TWINS):
+            chunks = range(e0 * PASSES, (e0 + TWINS) * PASSES)
+            raws = [load_w(k) for k in chunks]
+            if e0 + TWINS == E:
                 rows = wp.rearrange("(c t i) f -> t c i f", t=PACK, i=4)
                 for t in range(PACK):
                     nc.sync.dma_start(wpraw[:, t, :], rows[t])
-                load_gates(e - 1, E)
-                last = [quantize_w(e * PASSES + a, raws[a]) for a in range(PASSES)]
-                finish(e - 1, quantized)
-                finish(e, last)
+            quantized = [quantize_w(k, raw) for k, raw in zip(chunks, raws)]
+            pairs = [raws[LAST][:, u * TWINS * C:(u + 1) * TWINS * C] for u in range(HALVES)]
+            for e in range(e0, e0 + TWINS):
+                expert(e, quantized[(e - e0) * PASSES:(e - e0 + 1) * PASSES], pairs)
+            scatter(e0 * C, (e0 + TWINS) * C, pairs)
 
         quantize_wp()
         woven_last = weave_on_scalar(*TOKEN_CHUNKS[-1])

@@ -24,7 +24,10 @@ KP = P * PACK
 PASSES = K // KP
 HALVES = 2
 F_BLOCKS = M // P
-X_COPIES = ((0, 512, "v"), (768, 1280, "s"), (512, 768, "v"))
+X_COPIES = (
+    ((0, 512, "v"), (640, 768, "s"), (768, 1280, "s"), (512, 640, "v")),
+    ((0, 512, "v"), (768, 1280, "s"), (512, 768, "v")),
+)
 X_QUANTIZE = ((0, 512), (512, 768), (768, 1280))
 GATHERS = ((0, 512), (512, 1024))
 TWINS = 2
@@ -33,7 +36,10 @@ VECTOR_SHARE = 2
 BANK = 512
 BLOCK = 256
 ZEROS = T // BLOCK
-TOKEN_CHUNKS = ((0, 256), (256, 512), (512, 768), (768, 1280))
+FIRST = (0, 128)
+SECOND = ((768, 1024), (1024, 1280))
+WOVEN_AT = {768: 0, 0: 512, 256: 768, 128: 1280, 1024: 1536}
+THIRD = ((128, 256), (256, 512), (512, 768))
 
 
 def tile_moe_nxt_lin_none_kernel(tc, xT, w, wp, gate, offs, out):
@@ -44,9 +50,7 @@ def tile_moe_nxt_lin_none_kernel(tc, xT, w, wp, gate, offs, out):
         wraw = ctx.enter_context(tc.tile_pool(name="wraw", bufs=4))
         wbf = ctx.enter_context(tc.tile_pool(name="wbf", bufs=4))
         wq = ctx.enter_context(tc.tile_pool(name="wq", bufs=6))
-        cpool = ctx.enter_context(tc.tile_pool(name="c", bufs=3))
-        ypsum = ctx.enter_context(tc.psum_pool(name="ypsum", bufs=2))
-        opsum = ctx.enter_context(tc.psum_pool(name="opsum", bufs=4))
+        psum = ctx.enter_context(tc.psum_pool(name="psum", bufs=8))
 
         offsets = keep.tile([P, SLOTS // 16], U16, name="offsets")
         xcodes = [keep.tile([P, T], U32, align_bytes=64, name="xcodes%d" % a) for a in range(PASSES)]
@@ -57,7 +61,8 @@ def tile_moe_nxt_lin_none_kernel(tc, xT, w, wp, gate, offs, out):
         gate_rows = keep.tile([P, C], F32, name="gate_rows")
         gate_columns = keep.tile([P, E], F32, name="gate_columns")
         spread = keep.tile([P, E, C], F32, name="spread")
-        wpraw = keep.tile([P, PACK, M], F32, name="wpraw")
+        wproom = keep.tile([P, 8 * BLOCK], F32, align_bytes=64, name="wproom")
+        wpraw = wproom[:, BLOCK:BLOCK + PACK * M].rearrange("p (t f) -> p t f", t=PACK)
         wpbf = keep.tile([P, M, PACK], BF16, align_bytes=64, name="wpbf")
         wpcodes = keep.tile([P, M], U32, align_bytes=64, name="wpcodes")
         wpscales = keep.tile([P, M], U8, align_bytes=64, name="wpscales")
@@ -83,7 +88,7 @@ def tile_moe_nxt_lin_none_kernel(tc, xT, w, wp, gate, offs, out):
             if a == 0:
                 nc.sync.dma_start(offsets[:], offs)
             rows = xr[:].rearrange("p (j t) -> p j t", j=PACK)
-            for t0, t1, engine in X_COPIES:
+            for t0, t1, engine in X_COPIES[a]:
                 copy(
                     engine,
                     xb[:, t0 * PACK:t1 * PACK].rearrange("p (c i j) -> p c j i", i=4, j=PACK),
@@ -115,7 +120,7 @@ def tile_moe_nxt_lin_none_kernel(tc, xT, w, wp, gate, offs, out):
             grouped = wbf.tile([P, N * PACK], BF16, align_bytes=64, name="grouped")
             dst = grouped[:].rearrange("p (t c i j) -> p t c j i", t=PACK, i=4, j=PACK)
             src = raw[:].rearrange("p (j c t i) -> p t c j i", j=PACK, t=PACK, i=4)
-            split = VECTOR_SHARE if k % (LAST + 1) == LAST else 0
+            split = VECTOR_SHARE if k % (LAST + 1) == LAST and k != LAST else 0
             if split:
                 copy("v", dst[:, 0:split], src[:, 0:split])
             copy("s", dst[:, split:PACK], src[:, split:PACK])
@@ -133,7 +138,7 @@ def tile_moe_nxt_lin_none_kernel(tc, xT, w, wp, gate, offs, out):
         def expert(e, quantized, pairs):
             cols = slice(e * C, (e + 1) * C)
             for u in range(HALVES):
-                y = ypsum.tile([P, 2, C], F32, name="y%d" % u)
+                y = psum.tile([P, 2, C], F32, name="bank")
                 for i in range(2):
                     t = 2 * u + i
                     for a in range(PASSES):
@@ -158,11 +163,11 @@ def tile_moe_nxt_lin_none_kernel(tc, xT, w, wp, gate, offs, out):
             make_identity(nc, identity[:])
             nc.gpsimd.memset(gate_rows[:], 0.0)
             nc.sync.dma_start(gate_rows[0:E, :], gate[0, :].rearrange("(e s) -> e s", s=C))
-            turned = opsum.tile([P, P], F32, name="bank")
+            turned = psum.tile([P, P], F32, name="bank")
             nc.tensor.transpose(turned[:], gate_rows[:], identity[:])
             nc.scalar.copy(out=gate_columns[:], in_=turned[:, 0:E])
             for e0 in range(0, E, BANK // C):
-                bank = opsum.tile([P, BANK // C, C], F32, name="bank")
+                bank = psum.tile([P, BANK // C, C], F32, name="bank")
                 for e in range(e0, e0 + BANK // C):
                     nc.tensor.transpose(bank[:, e - e0, :], gate_columns[:, e:e + 1].to_broadcast([P, P]), identity[:])
                 nc.scalar.copy(out=spread[:, e0:e0 + BANK // C, :], in_=bank[:])
@@ -172,20 +177,23 @@ def tile_moe_nxt_lin_none_kernel(tc, xT, w, wp, gate, offs, out):
                 nc.vector.tensor_copy(out=windows[u][:].indirect(offsets_of(s0, s1)), in_=pairs[u])
 
         def quantize_wp():
-            for f0, f1 in ((0, 128), (128, 256), (256, M)):
-                copy(
-                    "s",
-                    wpbf[:, f0:f1, :].rearrange("q (c i) r -> q c r i", i=4),
-                    wpraw[:, :, f0:f1].rearrange("q r (c i) -> q c r i", i=4),
-                )
+            copy(
+                "s",
+                wpbf[:].rearrange("q (c i) r -> q c r i", i=4),
+                wpraw.rearrange("q r (c i) -> q c r i", i=4),
+            )
+            for f0, f1 in ((0, 256), (256, M)):
                 nc.vector.quantize_mx(
                     out=wpcodes[:, f0:f1].bitcast(FP8X4),
                     scales=wpscales[:, f0:f1],
                     in_=wpbf[:, f0:f1, :].rearrange("p f r -> p (f r)"),
                 )
 
-        def weave(t0, t1):
-            woven = cpool.tile([P, (t1 - t0) * PACK], BF16, align_bytes=64, name="woven")
+        def woven_tile(t0, t1):
+            start = WOVEN_AT[t0]
+            return wproom[:, start:start + (t1 - t0) * HALVES].bitcast(BF16)
+
+        def weave(woven, t0, t1):
             b = t0 // BLOCK
             picks = (slice(b, ZEROS + 1, ZEROS - b), slice(ZEROS, b - 1 if b else None, b - ZEROS))
             halves = [
@@ -196,42 +204,41 @@ def tile_moe_nxt_lin_none_kernel(tc, xT, w, wp, gate, offs, out):
                 for u in range(HALVES)
             ]
             nc.vector.tensor_tensor(
-                out=woven[:].rearrange("p (s u i) -> p s u i", u=HALVES, i=2), in0=halves[0], in1=halves[1], op=ADD
+                out=woven.rearrange("p (s u i) -> p s u i", u=HALVES, i=2), in0=halves[0], in1=halves[1], op=ADD
             )
-            return woven
 
-        def project(woven, t0, t1):
-            width = t1 - t0
-            ccodes = cpool.tile([P, width], U32, align_bytes=64, name="ccodes")
-            cscales = cpool.tile([P, width], U8, align_bytes=64, name="cscales")
-            nc.vector.quantize_mx(out=ccodes[:].bitcast(FP8X4), scales=cscales[:], in_=woven[:])
-            staged = keep.tile([P, F_BLOCKS, width], F32, name="staged%d" % t0)
-            rows = out[:, t0:t1].rearrange("(f p) t -> p f t", p=P)
-            for f0 in range(0, F_BLOCKS, BANK // width):
-                f1 = min(f0 + BANK // width, F_BLOCKS)
-                bank = opsum.tile([P, f1 - f0, width], F32, name="bank")
-                for f in range(f0, f1):
-                    nc.tensor.matmul_mx(
-                        out=bank[:, f - f0, :],
-                        lhsT=wpcodes[:, f * P:(f + 1) * P].bitcast(FP8X4),
-                        lhsT_scale=wpscales[:, f * P:(f + 1) * P],
-                        rhs=ccodes[:].bitcast(FP8X4),
-                        rhs_scale=cscales[:],
-                        start=True,
-                        stop=True,
-                    )
-                copy("v" if width == BANK and f0 == 1 else "s", staged[:, f0:f1, :], bank[:])
-                if width == BANK:
-                    nc.sync.dma_start(rows[:, f0:f1, :], staged[:, f0:f1, :])
-            if width < BANK:
-                nc.sync.dma_start(rows, staged[:])
+        def quantize_c(woven, t0, t1):
+            ccodes = keep.tile([P, t1 - t0], U32, align_bytes=64, name="ccodes%d" % t0)
+            cscales = keep.tile([P, t1 - t0], U8, align_bytes=64, name="cscales%d" % t0)
+            nc.vector.quantize_mx(out=ccodes[:].bitcast(FP8X4), scales=cscales[:], in_=woven)
+            return ccodes, cscales
 
-        def weave_on_scalar(t0, t1):
-            woven = keep.tile([P, (t1 - t0) * PACK], BF16, align_bytes=64, name="woven_last")
-            words = woven[:].bitcast(F32).rearrange("p (s u) -> p s u", u=HALVES)
-            for u in range(HALVES):
-                nc.scalar.copy(out=words[:, :, u], in_=windows[u][:, t0:t1])
-            return woven
+        def project(dst, f, quantized):
+            ccodes, cscales = quantized
+            nc.tensor.matmul_mx(
+                out=dst,
+                lhsT=wpcodes[:, f * P:(f + 1) * P].bitcast(FP8X4),
+                lhsT_scale=wpscales[:, f * P:(f + 1) * P],
+                rhs=ccodes[:].bitcast(FP8X4),
+                rhs_scale=cscales[:],
+                start=True,
+                stop=True,
+            )
+
+        def project_narrow(engine, dst, quantized):
+            bank = psum.tile([P, F_BLOCKS, P], F32, name="bank")
+            for f in range(F_BLOCKS):
+                project(bank[:, f, :], f, quantized)
+            copy(engine, dst, bank[:])
+
+        def project_wide(engine, dst, f, blocks):
+            bank = psum.tile([P, BANK], F32, name="bank")
+            for b, quantized in enumerate(blocks):
+                project(bank[:, b * BLOCK:(b + 1) * BLOCK], f, quantized)
+            copy(engine, dst, bank[:])
+
+        def store(staged, f, t0, t1):
+            nc.sync.dma_start(out[f * P:(f + 1) * P, t0:t1], staged)
 
         spread_gates()
         quantize_x(0)
@@ -256,7 +263,30 @@ def tile_moe_nxt_lin_none_kernel(tc, xT, w, wp, gate, offs, out):
             scatter(e0 * C, (e0 + TWINS) * C, pairs)
 
         quantize_wp()
-        woven_last = weave_on_scalar(*TOKEN_CHUNKS[-1])
-        for t0, t1 in TOKEN_CHUNKS[:-1]:
-            project(weave(t0, t1), t0, t1)
-        project(woven_last, *TOKEN_CHUNKS[-1])
+        second = [woven_tile(*tokens) for tokens in SECOND]
+        for u in range(HALVES):
+            for woven, (t0, t1) in zip(second, SECOND):
+                words = woven.bitcast(F32).rearrange("p (s u) -> p s u", u=HALVES)
+                nc.scalar.copy(out=words[:, :, u], in_=windows[u][:, t0:t1])
+
+        first = woven_tile(*FIRST)
+        weave(first, *FIRST)
+        staged = keep.tile([P, F_BLOCKS, P], F32, name="staged_first")
+        project_narrow("s", staged[:], quantize_c(first, *FIRST))
+        nc.sync.dma_start(out[:, FIRST[0]:FIRST[1]].rearrange("(f p) t -> p f t", p=P), staged[:])
+
+        blocks = [quantize_c(woven, *tokens) for woven, tokens in zip(second, SECOND)]
+        for f in range(F_BLOCKS):
+            staged = keep.tile([P, BANK], F32, name="staged_second%d" % f)
+            project_wide("s", staged[:], f, blocks)
+            store(staged[:], f, SECOND[0][0], SECOND[-1][1])
+
+        third = [woven_tile(*THIRD[0]), woven_tile(*THIRD[1]), second[0]]
+        for woven, tokens in zip(third, THIRD):
+            weave(woven, *tokens)
+        blocks = [quantize_c(woven, *tokens) for woven, tokens in zip(third, THIRD)]
+        staged = keep.tile([P, F_BLOCKS, P + BANK], F32, name="staged_third")
+        project_narrow("v", staged[:, :, 0:P], blocks[0])
+        for f in range(F_BLOCKS):
+            project_wide("v" if f == 1 else "s", staged[:, f, P:P + BANK], f, blocks[1:])
+            store(staged[:, f, :], f, THIRD[0][0], THIRD[-1][1])

@@ -120,7 +120,7 @@ def tile_moe_nxt_lin_none_kernel(tc, xT, w, wp, gate, offs, out):
             grouped = wbf.tile([P, N * PACK], BF16, align_bytes=64, name="grouped")
             dst = grouped[:].rearrange("p (t c i j) -> p t c j i", t=PACK, i=4, j=PACK)
             src = raw[:].rearrange("p (j c t i) -> p t c j i", j=PACK, t=PACK, i=4)
-            split = VECTOR_SHARE if k % (LAST + 1) == LAST and k != LAST else 0
+            split = VECTOR_SHARE if k == E * PASSES - 1 else 0
             if split:
                 copy("v", dst[:, 0:split], src[:, 0:split])
             copy("s", dst[:, split:PACK], src[:, split:PACK])

@@ -34,6 +34,7 @@ TWINS = 2
 LAST = TWINS * PASSES - 1
 VECTOR_SHARE = 2
 BANK = 512
+SPARE = 128
 BLOCK = 256
 ZEROS = T // BLOCK
 FIRST = (0, 128)
@@ -53,8 +54,8 @@ def tile_moe_nxt_lin_none_kernel(tc, xT, w, wp, gate, offs, out):
         psum = ctx.enter_context(tc.psum_pool(name="psum", bufs=8))
 
         offsets = keep.tile([P, SLOTS // 16], U16, name="offsets")
-        xcodes = [keep.tile([P, T], U32, align_bytes=64, name="xcodes%d" % a) for a in range(PASSES)]
-        xscales = keep.tile([P, T], U8, align_bytes=64, name="xscales")
+        xcodes = [keep.tile([P, T + a * SPARE], U32, align_bytes=64, name="xcodes%d" % a) for a in range(PASSES)]
+        xscales = keep.tile([P, T + SPARE], U8, align_bytes=64, name="xscales")
         gcodes = [keep.tile([P, SLOTS], U32, align_bytes=64, name="gcodes%d" % a) for a in range(PASSES)]
         gscales = keep.tile([P, SLOTS], U8, align_bytes=64, name="gscales")
         identity = keep.tile([P, P], F32, name="identity")
@@ -69,6 +70,7 @@ def tile_moe_nxt_lin_none_kernel(tc, xT, w, wp, gate, offs, out):
         windows = [keep.tile([P, T + BLOCK], F32, name="window%d" % u) for u in range(HALVES)]
 
         nc.vector.memset(xscales[:].bitcast(I32), 0)
+        nc.vector.memset(xcodes[1][:, T:].bitcast(I32), 0)
         for u in range(HALVES):
             nc.vector.memset(windows[u][:], 0.0)
 
@@ -159,6 +161,29 @@ def tile_moe_nxt_lin_none_kernel(tc, xT, w, wp, gate, offs, out):
                     op=MULT,
                 )
 
+        def first_twin(e, quantized, room):
+            cols = slice(e * C, (e + 1) * C)
+            y = psum.tile([P, PACK, C], F32, name="bank")
+            for t in range(PACK):
+                for a in range(PASSES):
+                    codes, scales = quantized[a]
+                    nc.tensor.matmul_mx(
+                        out=y[:, t, :],
+                        lhsT=codes[:, t * P:(t + 1) * P].bitcast(FP8X4),
+                        lhsT_scale=scales[:, t * P:(t + 1) * P],
+                        rhs=gcodes[a][:, cols].bitcast(FP8X4),
+                        rhs_scale=gscales[PACK * a:P, cols],
+                        start=(a == 0),
+                        stop=(a == PASSES - 1),
+                    )
+            planes = room[:, 0:HALVES * TWINS * C].bitcast(BF16).rearrange("p (u s i) -> p u s i", u=HALVES, i=2)
+            nc.vector.tensor_tensor(
+                out=planes[:, :, 0:C, :],
+                in0=y[:].rearrange("p (u i) s -> p u s i", u=HALVES),
+                in1=spread[:, e, :].unsqueeze(1).unsqueeze(3).to_broadcast([P, HALVES, C, 2]),
+                op=MULT,
+            )
+
         def spread_gates():
             make_identity(nc, identity[:])
             nc.gpsimd.memset(gate_rows[:], 0.0)
@@ -245,9 +270,8 @@ def tile_moe_nxt_lin_none_kernel(tc, xT, w, wp, gate, offs, out):
         for s0, s1 in GATHERS:
             gather_codes(0, s0, s1)
         quantize_x(1)
-        for s0, s1 in GATHERS:
-            gather_codes(1, s0, s1)
-            gather_scales(s0, s1)
+        gather_codes(1, 0, SLOTS)
+        gather_scales(0, SLOTS)
 
         for e0 in range(0, E, TWINS):
             chunks = range(e0 * PASSES, (e0 + TWINS) * PASSES)
@@ -258,8 +282,8 @@ def tile_moe_nxt_lin_none_kernel(tc, xT, w, wp, gate, offs, out):
                     nc.sync.dma_start(wpraw[:, t, :], rows[t])
             quantized = [quantize_w(k, raw) for k, raw in zip(chunks, raws)]
             pairs = [raws[LAST][:, u * TWINS * C:(u + 1) * TWINS * C] for u in range(HALVES)]
-            for e in range(e0, e0 + TWINS):
-                expert(e, quantized[(e - e0) * PASSES:(e - e0 + 1) * PASSES], pairs)
+            first_twin(e0, quantized[0:PASSES], raws[LAST])
+            expert(e0 + 1, quantized[PASSES:], pairs)
             scatter(e0 * C, (e0 + TWINS) * C, pairs)
 
         quantize_wp()

@@ -49,8 +49,8 @@ def tile_moe_nxt_lin_none_kernel(tc, xT, w, wp, gate, offs, out):
         keep = ctx.enter_context(tc.tile_pool(name="keep", bufs=1))
         xbf = ctx.enter_context(tc.tile_pool(name="xbf", bufs=PASSES))
         wraw = ctx.enter_context(tc.tile_pool(name="wraw", bufs=4))
-        wbf = ctx.enter_context(tc.tile_pool(name="wbf", bufs=4))
-        wq = ctx.enter_context(tc.tile_pool(name="wq", bufs=6))
+        wbf = ctx.enter_context(tc.tile_pool(name="wbf", bufs=2))
+        wq = ctx.enter_context(tc.tile_pool(name="wq", bufs=3))
         psum = ctx.enter_context(tc.psum_pool(name="psum", bufs=8))
 
         offsets = keep.tile([P, SLOTS // 16], U16, name="offsets")
@@ -118,14 +118,17 @@ def tile_moe_nxt_lin_none_kernel(tc, xT, w, wp, gate, offs, out):
             nc.sync.dma_start(raw[:], w[e, a * KP:(a + 1) * KP, :].rearrange("(p j) n -> p (j n)", j=PACK))
             return raw
 
-        def quantize_w(k, raw):
-            grouped = wbf.tile([P, N * PACK], BF16, align_bytes=64, name="grouped")
-            dst = grouped[:].rearrange("p (t c i j) -> p t c j i", t=PACK, i=4, j=PACK)
+        def round_w(k, raw, grouped):
+            dst = grouped.rearrange("p (t c i j) -> p t c j i", t=PACK, i=4, j=PACK)
             src = raw[:].rearrange("p (j c t i) -> p t c j i", j=PACK, t=PACK, i=4)
             split = VECTOR_SHARE if k == E * PASSES - 1 else 0
             if split:
                 copy("v", dst[:, 0:split], src[:, 0:split])
             copy("s", dst[:, split:PACK], src[:, split:PACK])
+
+        def quantize_w(k, raw):
+            grouped = wbf.tile([P, N * PACK], BF16, align_bytes=64, name="grouped")
+            round_w(k, raw, grouped[:])
             codes = wq.tile([P, N], U32, align_bytes=64, name="codes")
             scales = wq.tile([P, N], U8, align_bytes=64, name="scales")
             width = N // HALVES if k % (LAST + 1) == LAST else N
@@ -135,7 +138,16 @@ def tile_moe_nxt_lin_none_kernel(tc, xT, w, wp, gate, offs, out):
                     scales=scales[:, n0:n0 + width],
                     in_=grouped[:, n0 * PACK:(n0 + width) * PACK],
                 )
-            return codes, scales
+            return codes[:], scales[:]
+
+        def quantize_both(k, raws):
+            grouped = wbf.tile([P, PASSES * N * PACK], BF16, align_bytes=64, name="grouped_both")
+            for a in range(PASSES):
+                round_w(k + a, raws[a], grouped[:, a * N * PACK:(a + 1) * N * PACK])
+            codes = wq.tile([P, PASSES * N], U32, align_bytes=64, bufs=2, name="codes_both")
+            scales = wq.tile([P, PASSES * N], U8, align_bytes=64, bufs=2, name="scales_both")
+            nc.vector.quantize_mx(out=codes[:].bitcast(FP8X4), scales=scales[:], in_=grouped[:])
+            return [(codes[:, a * N:(a + 1) * N], scales[:, a * N:(a + 1) * N]) for a in range(PASSES)]
 
         def expert(e, quantized, pairs):
             cols = slice(e * C, (e + 1) * C)
@@ -280,7 +292,8 @@ def tile_moe_nxt_lin_none_kernel(tc, xT, w, wp, gate, offs, out):
                 rows = wp.rearrange("(c t i) f -> t c i f", t=PACK, i=4)
                 for t in range(PACK):
                     nc.sync.dma_start(wpraw[:, t, :], rows[t])
-            quantized = [quantize_w(k, raw) for k, raw in zip(chunks, raws)]
+            quantized = quantize_both(chunks[0], raws[0:PASSES])
+            quantized.extend(quantize_w(k, raw) for k, raw in zip(chunks[PASSES:], raws[PASSES:]))
             pairs = [raws[LAST][:, u * TWINS * C:(u + 1) * TWINS * C] for u in range(HALVES)]
             first_twin(e0, quantized[0:PASSES], raws[LAST])
             expert(e0 + 1, quantized[PASSES:], pairs)

@@ -153,18 +153,19 @@ def tile_moe_nxt_lin_none_kernel(tc, xT, w, wp, gate, offs, out):
             cols = slice(e * C, (e + 1) * C)
             for u in range(HALVES):
                 y = psum.tile([P, 2, C], F32, name="bank")
-                for i in range(2):
-                    t = 2 * u + i
-                    for a in range(PASSES):
-                        codes, scales = quantized[a]
+                joined = e == E - 1
+                steps = [(a, i) for i in range(2) for a in range(PASSES)]
+                for a, i in sorted(steps) if joined else steps:
+                    codes, scales = quantized[a]
+                    for t in (2 * u + i,):
                         nc.tensor.matmul_mx(
                             out=y[:, i, :],
                             lhsT=codes[:, t * P:(t + 1) * P].bitcast(FP8X4),
                             lhsT_scale=scales[:, t * P:(t + 1) * P],
                             rhs=gcodes[a][:, cols].bitcast(FP8X4),
                             rhs_scale=gscales[PACK * a:P, cols],
-                            start=(a == 0),
-                            stop=(a == PASSES - 1),
+                            start=(a == 0 and (i == 0 or not joined)),
+                            stop=(a == PASSES - 1 and (i == 1 or not joined)),
                         )
                 nc.vector.tensor_tensor(
                     out=pairs[u][:, e % TWINS * C:(e % TWINS + 1) * C].bitcast(BF16).rearrange("p (s i) -> p s i", i=2),

@@ -17,12 +17,13 @@ U8 = mybir.dt.uint8
 FP8X4 = mybir.dt.float8_e4m3fn_x4
 ADD = mybir.AluOpType.add
 MULT = mybir.AluOpType.mult
+COPY = mybir.ActivationFunctionType.Copy
 
 P = 128
 PACK = 4
 KP = P * PACK
 PASSES = K // KP
-HALVES = 2
+CHUNKS = E * PASSES
 F_BLOCKS = M // P
 X_COPIES = (
     ((0, 512, "v"), (640, 768, "s"), (768, 1280, "s"), (512, 640, "v")),
@@ -30,27 +31,28 @@ X_COPIES = (
 )
 X_QUANTIZE = ((0, 512), (512, 768), (768, 1280))
 GATHERS = ((0, 512), (512, 1024))
-TWINS = 2
-LAST = TWINS * PASSES - 1
-VECTOR_SHARE = 2
+VECTOR_QUARTERS = (0, 0, 0, 2, 0, 4, 3, 4, 3, 4, 3, 4, 3, 4, 3, 2)
 BANK = 512
 SPARE = 128
-BLOCK = 256
-ZEROS = T // BLOCK
-FIRST = (0, 128)
-SECOND = ((768, 1024), (1024, 1280))
-WOVEN_AT = {768: 0, 0: 512, 256: 768, 128: 1280, 1024: 1536}
-THIRD = ((128, 256), (256, 512), (512, 768))
+EARLY_SCATTERS = {
+    1: ((0, 0, 192), (1, 0, 192), (2, 0, 192)),
+    2: ((0, 192, 384), (1, 192, 384), (2, 192, 384)),
+    4: ((0, 384, 576), (1, 384, 576), (2, 384, 640)),
+    5: ((0, 576, 768), (1, 576, 768)),
+}
+LATE = E - 3
 
 
 def tile_moe_nxt_lin_none_kernel(tc, xT, w, wp, gate, offs, out):
     nc = tc.nc
     with ExitStack() as ctx:
+        rows = ctx.enter_context(tc.tile_pool(name="rows", bufs=1))
+        wraw = ctx.enter_context(tc.tile_pool(name="wraw", bufs=5))
         keep = ctx.enter_context(tc.tile_pool(name="keep", bufs=1))
         xbf = ctx.enter_context(tc.tile_pool(name="xbf", bufs=PASSES))
-        wraw = ctx.enter_context(tc.tile_pool(name="wraw", bufs=4))
-        wbf = ctx.enter_context(tc.tile_pool(name="wbf", bufs=2))
+        wbf = ctx.enter_context(tc.tile_pool(name="wbf", bufs=3))
         wq = ctx.enter_context(tc.tile_pool(name="wq", bufs=3))
+        cq = ctx.enter_context(tc.tile_pool(name="cq", bufs=3))
         psum = ctx.enter_context(tc.psum_pool(name="psum", bufs=8))
 
         offsets = keep.tile([P, SLOTS // 16], U16, name="offsets")
@@ -62,17 +64,19 @@ def tile_moe_nxt_lin_none_kernel(tc, xT, w, wp, gate, offs, out):
         gate_rows = keep.tile([P, C], F32, name="gate_rows")
         gate_columns = keep.tile([P, E], F32, name="gate_columns")
         spread = keep.tile([P, E, C], F32, name="spread")
-        wproom = keep.tile([P, 8 * BLOCK], F32, align_bytes=64, name="wproom")
-        wpraw = wproom[:, BLOCK:BLOCK + PACK * M].rearrange("p (t f) -> p t f", t=PACK)
+        wpraw = rows.tile([P, PACK, M], F32, align_bytes=256, name="wpraw")
         wpbf = keep.tile([P, M, PACK], BF16, align_bytes=64, name="wpbf")
         wpcodes = keep.tile([P, M], U32, align_bytes=64, name="wpcodes")
         wpscales = keep.tile([P, M], U8, align_bytes=64, name="wpscales")
-        windows = [keep.tile([P, T + BLOCK], F32, name="window%d" % u) for u in range(HALVES)]
+        windows = [rows.tile([P, T], F32, align_bytes=256, name="window%d" % f) for f in range(F_BLOCKS)]
+        staged = keep.tile([P, F_BLOCKS, (LATE + 1) * C], F32, name="staged")
+        zeros = keep.tile([P, C], F32, name="zeros")
 
         nc.vector.memset(xscales[:].bitcast(I32), 0)
         nc.vector.memset(xcodes[1][:, T:].bitcast(I32), 0)
-        for u in range(HALVES):
-            nc.vector.memset(windows[u][:], 0.0)
+        nc.vector.memset(zeros[:], 0.0)
+        for f in range(F_BLOCKS):
+            nc.vector.memset(windows[f][:], 0.0)
 
         def copy(engine, dst, src):
             if engine == "v":
@@ -85,16 +89,16 @@ def tile_moe_nxt_lin_none_kernel(tc, xT, w, wp, gate, offs, out):
 
         def quantize_x(a):
             xb = xbf.tile([P, T * PACK], BF16, align_bytes=64, name="xb")
-            xr = keep.tile([P, PACK * T], F32, name="xr%d" % a)
+            xr = rows.tile([P, PACK * T], F32, align_bytes=256, name="xr%d" % a)
             nc.sync.dma_start(xr[:], xT[a * KP:(a + 1) * KP, :].rearrange("(p j) t -> p (j t)", j=PACK))
             if a == 0:
                 nc.sync.dma_start(offsets[:], offs)
-            rows = xr[:].rearrange("p (j t) -> p j t", j=PACK)
+            lines = xr[:].rearrange("p (j t) -> p j t", j=PACK)
             for t0, t1, engine in X_COPIES[a]:
                 copy(
                     engine,
                     xb[:, t0 * PACK:t1 * PACK].rearrange("p (c i j) -> p c j i", i=4, j=PACK),
-                    rows[:, :, t0:t1].rearrange("p j (c i) -> p c j i", i=4),
+                    lines[:, :, t0:t1].rearrange("p j (c i) -> p c j i", i=4),
                 )
             for q0, q1 in X_QUANTIZE:
                 nc.vector.quantize_mx(
@@ -111,91 +115,89 @@ def tile_moe_nxt_lin_none_kernel(tc, xT, w, wp, gate, offs, out):
 
         def load_w(k):
             e, a = divmod(k, PASSES)
-            if k % (LAST + 1) == LAST:
-                raw = keep.tile([P, PACK * N], F32, name="raw%d" % k)
+            if k == CHUNKS - 1:
+                raw = rows.tile([P, PACK * N], F32, align_bytes=256, name="raw_last")
             else:
-                raw = wraw.tile([P, PACK * N], F32, name="raw")
+                raw = wraw.tile([P, PACK * N], F32, align_bytes=256, name="raw")
             nc.sync.dma_start(raw[:], w[e, a * KP:(a + 1) * KP, :].rearrange("(p j) n -> p (j n)", j=PACK))
             return raw
 
-        def round_w(k, raw, grouped):
-            dst = grouped.rearrange("p (t c i j) -> p t c j i", t=PACK, i=4, j=PACK)
-            src = raw[:].rearrange("p (j c t i) -> p t c j i", j=PACK, t=PACK, i=4)
-            split = VECTOR_SHARE if k == E * PASSES - 1 else 0
-            if split:
-                copy("v", dst[:, 0:split], src[:, 0:split])
-            copy("s", dst[:, split:PACK], src[:, split:PACK])
+        def round_w(k, raw, dst):
+            src = raw[:].rearrange("p (j c t i) -> p c t j i", j=PACK, t=PACK, i=4)
+            share = VECTOR_QUARTERS[k]
+            if share == PACK:
+                for t0 in (0, 2):
+                    copy("v", dst[:, :, t0:t0 + 2], src[:, :, t0:t0 + 2])
+                return
+            if share:
+                copy("v", dst[:, :, 0:share], src[:, :, 0:share])
+            copy("s", dst[:, :, share:PACK], src[:, :, share:PACK])
 
-        def quantize_w(k, raw):
-            grouped = wbf.tile([P, N * PACK], BF16, align_bytes=64, name="grouped")
-            round_w(k, raw, grouped[:])
-            codes = wq.tile([P, N], U32, align_bytes=64, name="codes")
-            scales = wq.tile([P, N], U8, align_bytes=64, name="scales")
-            width = N // HALVES if k % (LAST + 1) == LAST else N
-            for n0 in range(0, N, width):
+        def quantize_w(e, raws):
+            last = e == E - 1
+            order = "(a t" if last else "(t a"
+            grouped = wbf.tile([P, PASSES * N * PACK], BF16, align_bytes=64, name="grouped")
+            codes = wq.tile([P, PASSES * N], U32, align_bytes=64, name="codes")
+            scales = wq.tile([P, PASSES * N], U8, align_bytes=64, name="scales")
+            dst = grouped[:].rearrange("p " + order + " c i j) -> p a c t j i", a=PASSES, t=PACK, i=4, j=PACK)
+            width = N // 2 if last else N
+
+            def quantize(n0):
                 nc.vector.quantize_mx(
                     out=codes[:, n0:n0 + width].bitcast(FP8X4),
                     scales=scales[:, n0:n0 + width],
                     in_=grouped[:, n0 * PACK:(n0 + width) * PACK],
                 )
-            return codes[:], scales[:]
 
-        def quantize_both(k, raws):
-            grouped = wbf.tile([P, PASSES * N * PACK], BF16, align_bytes=64, name="grouped_both")
             for a in range(PASSES):
-                round_w(k + a, raws[a], grouped[:, a * N * PACK:(a + 1) * N * PACK])
-            codes = wq.tile([P, PASSES * N], U32, align_bytes=64, bufs=2, name="codes_both")
-            scales = wq.tile([P, PASSES * N], U8, align_bytes=64, bufs=2, name="scales_both")
-            nc.vector.quantize_mx(out=codes[:].bitcast(FP8X4), scales=scales[:], in_=grouped[:])
-            return [(codes[:, a * N:(a + 1) * N], scales[:, a * N:(a + 1) * N]) for a in range(PASSES)]
+                round_w(e * PASSES + a, raws[a], dst[:, a])
+            for n0 in range(0, PASSES * N, width):
+                quantize(n0)
+            pattern = "p " + order + " m) -> p a t m"
+            return codes[:].rearrange(pattern, a=PASSES, t=PACK), scales[:].rearrange(pattern, a=PASSES, t=PACK)
 
-        def expert(e, quantized, pairs):
-            cols = slice(e * C, (e + 1) * C)
-            for u in range(HALVES):
-                y = psum.tile([P, 2, C], F32, name="bank")
-                joined = e == E - 1
-                steps = [(a, i) for i in range(2) for a in range(PASSES)]
-                for a, i in sorted(steps) if joined else steps:
-                    codes, scales = quantized[a]
-                    for t in (2 * u + i,):
-                        nc.tensor.matmul_mx(
-                            out=y[:, i, :],
-                            lhsT=codes[:, t * P:(t + 1) * P].bitcast(FP8X4),
-                            lhsT_scale=scales[:, t * P:(t + 1) * P],
-                            rhs=gcodes[a][:, cols].bitcast(FP8X4),
-                            rhs_scale=gscales[PACK * a:P, cols],
-                            start=(a == 0 and (i == 0 or not joined)),
-                            stop=(a == PASSES - 1 and (i == 1 or not joined)),
-                        )
-                nc.vector.tensor_tensor(
-                    out=pairs[u][:, e % TWINS * C:(e % TWINS + 1) * C].bitcast(BF16).rearrange("p (s i) -> p s i", i=2),
-                    in0=y[:].rearrange("p i s -> p s i"),
-                    in1=spread[:, e, :].unsqueeze(2).to_broadcast([P, C, 2]),
-                    op=MULT,
-                )
-
-        def first_twin(e, quantized, room):
+        def expert(e, quantized):
             cols = slice(e * C, (e + 1) * C)
             y = psum.tile([P, PACK, C], F32, name="bank")
-            for t in range(PACK):
-                for a in range(PASSES):
-                    codes, scales = quantized[a]
-                    nc.tensor.matmul_mx(
-                        out=y[:, t, :],
-                        lhsT=codes[:, t * P:(t + 1) * P].bitcast(FP8X4),
-                        lhsT_scale=scales[:, t * P:(t + 1) * P],
-                        rhs=gcodes[a][:, cols].bitcast(FP8X4),
-                        rhs_scale=gscales[PACK * a:P, cols],
-                        start=(a == 0),
-                        stop=(a == PASSES - 1),
-                    )
-            planes = room[:, 0:HALVES * TWINS * C].bitcast(BF16).rearrange("p (u s i) -> p u s i", u=HALVES, i=2)
+            joined = e == E - 1
+            steps = [(a, t) for t in range(PACK) for a in range(PASSES)]
+            codes, scales = quantized
+            for a, t in sorted(steps) if joined else steps:
+                nc.tensor.matmul_mx(
+                    out=y[:, t, :],
+                    lhsT=codes[:, a, t, :].bitcast(FP8X4),
+                    lhsT_scale=scales[:, a, t, :],
+                    rhs=gcodes[a][:, cols].bitcast(FP8X4),
+                    rhs_scale=gscales[PACK * a:P, cols],
+                    start=(a == 0 and (t == 0 or not joined)),
+                    stop=(a == PASSES - 1 and (t == PACK - 1 or not joined)),
+                )
+            cb = cq.tile([P, C * PACK], BF16, align_bytes=64, name="cb")
             nc.vector.tensor_tensor(
-                out=planes[:, :, 0:C, :],
-                in0=y[:].rearrange("p (u i) s -> p u s i", u=HALVES),
-                in1=spread[:, e, :].unsqueeze(1).unsqueeze(3).to_broadcast([P, HALVES, C, 2]),
+                out=cb[:].rearrange("p (s t) -> p s t", t=PACK),
+                in0=y[:].rearrange("p t s -> p s t"),
+                in1=spread[:, e, :].unsqueeze(2).to_broadcast([P, C, PACK]),
                 op=MULT,
             )
+            ccodes = cq.tile([P, C], U32, align_bytes=64, name="ccodes")
+            cscales = cq.tile([P, C], U8, align_bytes=64, name="cscales")
+            nc.vector.quantize_mx(out=ccodes[:].bitcast(FP8X4), scales=cscales[:], in_=cb[:])
+            return ccodes, cscales
+
+        def project(f0, f1, quantized, dst, engine="s"):
+            ccodes, cscales = quantized
+            bank = psum.tile([P, f1 - f0, C], F32, name="bank")
+            for f in range(f0, f1):
+                nc.tensor.matmul_mx(
+                    out=bank[:, f - f0, :],
+                    lhsT=wpcodes[:, f * P:(f + 1) * P].bitcast(FP8X4),
+                    lhsT_scale=wpscales[:, f * P:(f + 1) * P],
+                    rhs=ccodes[:].bitcast(FP8X4),
+                    rhs_scale=cscales[:],
+                    start=True,
+                    stop=True,
+                )
+            copy(engine, dst, bank[:])
 
         def spread_gates():
             make_identity(nc, identity[:])
@@ -203,80 +205,36 @@ def tile_moe_nxt_lin_none_kernel(tc, xT, w, wp, gate, offs, out):
             nc.sync.dma_start(gate_rows[0:E, :], gate[0, :].rearrange("(e s) -> e s", s=C))
             turned = psum.tile([P, P], F32, name="bank")
             nc.tensor.transpose(turned[:], gate_rows[:], identity[:])
-            nc.scalar.copy(out=gate_columns[:], in_=turned[:, 0:E])
+            nc.scalar.activation(gate_columns[:], turned[:, 0:E], COPY)
             for e0 in range(0, E, BANK // C):
                 bank = psum.tile([P, BANK // C, C], F32, name="bank")
                 for e in range(e0, e0 + BANK // C):
                     nc.tensor.transpose(bank[:, e - e0, :], gate_columns[:, e:e + 1].to_broadcast([P, P]), identity[:])
                 nc.scalar.copy(out=spread[:, e0:e0 + BANK // C, :], in_=bank[:])
 
-        def scatter(s0, s1, pairs):
-            for u in range(HALVES):
-                nc.vector.tensor_copy(out=windows[u][:].indirect(offsets_of(s0, s1)), in_=pairs[u])
+        def scatter_scalar(f, s0, s1, values):
+            nc.scalar.activation(windows[f][:].indirect(offsets_of(s0, s1)), values, COPY)
+
+        def scatter_vector(f, e, values):
+            nc.vector.tensor_tensor(
+                out=windows[f][:].indirect(offsets_of(e * C, (e + 1) * C)), in0=values, in1=zeros[:], op=ADD
+            )
 
         def quantize_wp():
+            blocks = wp.rearrange("(c t i) f -> t c i f", t=PACK, i=4)
+            for t in range(PACK):
+                nc.sync.dma_start(wpraw[:, t, :], blocks[t])
             copy(
                 "s",
                 wpbf[:].rearrange("q (c i) r -> q c r i", i=4),
-                wpraw.rearrange("q r (c i) -> q c r i", i=4),
+                wpraw[:].rearrange("q r (c i) -> q c r i", i=4),
             )
-            for f0, f1 in ((0, 256), (256, M)):
-                nc.vector.quantize_mx(
-                    out=wpcodes[:, f0:f1].bitcast(FP8X4),
-                    scales=wpscales[:, f0:f1],
-                    in_=wpbf[:, f0:f1, :].rearrange("p f r -> p (f r)"),
-                )
-
-        def woven_tile(t0, t1):
-            start = WOVEN_AT[t0]
-            return wproom[:, start:start + (t1 - t0) * HALVES].bitcast(BF16)
-
-        def weave(woven, t0, t1):
-            b = t0 // BLOCK
-            picks = (slice(b, ZEROS + 1, ZEROS - b), slice(ZEROS, b - 1 if b else None, b - ZEROS))
-            halves = [
-                windows[u][:]
-                .bitcast(BF16)
-                .rearrange("p (b s i) -> p b s i", s=BLOCK, i=2)[:, picks[u], t0 - b * BLOCK:t1 - b * BLOCK, :]
-                .rearrange("p u s i -> p s u i")
-                for u in range(HALVES)
-            ]
-            nc.vector.tensor_tensor(
-                out=woven.rearrange("p (s u i) -> p s u i", u=HALVES, i=2), in0=halves[0], in1=halves[1], op=ADD
+            nc.vector.quantize_mx(
+                out=wpcodes[:].bitcast(FP8X4), scales=wpscales[:], in_=wpbf[:].rearrange("p f r -> p (f r)")
             )
 
-        def quantize_c(woven, t0, t1):
-            ccodes = keep.tile([P, t1 - t0], U32, align_bytes=64, name="ccodes%d" % t0)
-            cscales = keep.tile([P, t1 - t0], U8, align_bytes=64, name="cscales%d" % t0)
-            nc.vector.quantize_mx(out=ccodes[:].bitcast(FP8X4), scales=cscales[:], in_=woven)
-            return ccodes, cscales
-
-        def project(dst, f, quantized):
-            ccodes, cscales = quantized
-            nc.tensor.matmul_mx(
-                out=dst,
-                lhsT=wpcodes[:, f * P:(f + 1) * P].bitcast(FP8X4),
-                lhsT_scale=wpscales[:, f * P:(f + 1) * P],
-                rhs=ccodes[:].bitcast(FP8X4),
-                rhs_scale=cscales[:],
-                start=True,
-                stop=True,
-            )
-
-        def project_narrow(engine, dst, quantized):
-            bank = psum.tile([P, F_BLOCKS, P], F32, name="bank")
-            for f in range(F_BLOCKS):
-                project(bank[:, f, :], f, quantized)
-            copy(engine, dst, bank[:])
-
-        def project_wide(engine, dst, f, blocks):
-            bank = psum.tile([P, BANK], F32, name="bank")
-            for b, quantized in enumerate(blocks):
-                project(bank[:, b * BLOCK:(b + 1) * BLOCK], f, quantized)
-            copy(engine, dst, bank[:])
-
-        def store(staged, f, t0, t1):
-            nc.sync.dma_start(out[f * P:(f + 1) * P, t0:t1], staged)
+        def store(f):
+            nc.sync.dma_start(out[f * P:(f + 1) * P, :], windows[f][:])
 
         spread_gates()
         quantize_x(0)
@@ -285,46 +243,32 @@ def tile_moe_nxt_lin_none_kernel(tc, xT, w, wp, gate, offs, out):
         quantize_x(1)
         gather_codes(1, 0, SLOTS)
         gather_scales(0, SLOTS)
-
-        for e0 in range(0, E, TWINS):
-            chunks = range(e0 * PASSES, (e0 + TWINS) * PASSES)
-            raws = [load_w(k) for k in chunks]
-            if e0 + TWINS == E:
-                rows = wp.rearrange("(c t i) f -> t c i f", t=PACK, i=4)
-                for t in range(PACK):
-                    nc.sync.dma_start(wpraw[:, t, :], rows[t])
-            quantized = quantize_both(chunks[0], raws[0:PASSES])
-            quantized.extend(quantize_w(k, raw) for k, raw in zip(chunks[PASSES:], raws[PASSES:]))
-            pairs = [raws[LAST][:, u * TWINS * C:(u + 1) * TWINS * C] for u in range(HALVES)]
-            first_twin(e0, quantized[0:PASSES], raws[LAST])
-            expert(e0 + 1, quantized[PASSES:], pairs)
-            scatter(e0 * C, (e0 + TWINS) * C, pairs)
-
         quantize_wp()
-        second = [woven_tile(*tokens) for tokens in SECOND]
-        for u in range(HALVES):
-            for woven, (t0, t1) in zip(second, SECOND):
-                words = woven.bitcast(F32).rearrange("p (s u) -> p s u", u=HALVES)
-                nc.scalar.copy(out=words[:, :, u], in_=windows[u][:, t0:t1])
 
-        first = woven_tile(*FIRST)
-        weave(first, *FIRST)
-        staged = keep.tile([P, F_BLOCKS, P], F32, name="staged_first")
-        project_narrow("s", staged[:], quantize_c(first, *FIRST))
-        nc.sync.dma_start(out[:, FIRST[0]:FIRST[1]].rearrange("(f p) t -> p f t", p=P), staged[:])
+        def load_expert(e):
+            return [load_w(k) for k in range(e * PASSES, (e + 1) * PASSES)]
 
-        blocks = [quantize_c(woven, *tokens) for woven, tokens in zip(second, SECOND)]
-        for f in range(F_BLOCKS):
-            staged = keep.tile([P, BANK], F32, name="staged_second%d" % f)
-            project_wide("s", staged[:], f, blocks)
-            store(staged[:], f, SECOND[0][0], SECOND[-1][1])
+        for e in range(LATE + 1):
+            c = expert(e, quantize_w(e, load_expert(e)))
+            early = F_BLOCKS if e < LATE else F_BLOCKS - 1
+            project(0, early, c, staged[:, 0:early, e * C:(e + 1) * C])
+            for f, s0, s1 in EARLY_SCATTERS.get(e, ()):
+                scatter_scalar(f, s0, s1, staged[:, f, s0:s1])
 
-        third = [woven_tile(*THIRD[0]), woven_tile(*THIRD[1]), second[0]]
-        for woven, tokens in zip(third, THIRD):
-            weave(woven, *tokens)
-        blocks = [quantize_c(woven, *tokens) for woven, tokens in zip(third, THIRD)]
-        staged = keep.tile([P, F_BLOCKS, P + BANK], F32, name="staged_third")
-        project_narrow("v", staged[:, :, 0:P], blocks[0])
-        for f in range(F_BLOCKS):
-            project_wide("v" if f == 1 else "s", staged[:, f, P:P + BANK], f, blocks[1:])
-            store(staged[:, f, :], f, THIRD[0][0], THIRD[-1][1])
+        c6 = expert(E - 2, quantize_w(E - 2, load_expert(E - 2)))
+        raws = load_expert(E - 1)
+        quantized = quantize_w(E - 1, raws)
+        room = raws[-1][:, 0:F_BLOCKS * 3 * C].rearrange("p (f s) -> p f s", f=F_BLOCKS)
+        project(0, F_BLOCKS, c6, room[:, :, C:2 * C])
+        project(2, 3, c, room[:, 2:3, 0:C])
+        scatter_vector(0, E - 2, room[:, 0, C:2 * C])
+        scatter_scalar(2, LATE * C, (E - 1) * C, room[:, 2, 0:2 * C])
+        c7 = expert(E - 1, quantized)
+        project(0, 1, c7, room[:, 0:1, 2 * C:3 * C], "v")
+        project(1, F_BLOCKS, c7, room[:, 1:F_BLOCKS, 2 * C:3 * C])
+        scatter_vector(0, E - 1, room[:, 0, 2 * C:3 * C])
+        store(0)
+        scatter_scalar(1, (E - 2) * C, SLOTS, room[:, 1, C:3 * C])
+        store(1)
+        scatter_vector(2, E - 1, room[:, 2, 2 * C:3 * C])
+        store(2)

@@ -31,35 +31,43 @@ X_COPIES = (
 )
 X_QUANTIZE = ((0, 512), (512, 768), (768, 1280))
 GATHERS = ((0, 512), (512, 1024))
-VECTOR_QUARTERS = (0, 0, 0, 2, 0, 4, 3, 4, 3, 4, 3, 4, 3, 4, 3, 2)
+VECTOR_QUARTERS = (0, 0, 0, 2, 0, 2, 3, 4, 3, 4, 3, 3, 3, 3, 2, 2)
+BLOCKS = PASSES * PACK + 1
+CUTS_FIRST = ((1, 5), (5, 9))
+CUTS = ((0, 2), (2, 6), (6, 9))
+CUTS_LAST = ((0, 2), (2, 5), (5, 7), (7, 9))
 BANK = 512
 SPARE = 128
 EARLY_SCATTERS = {
-    1: ((0, 0, 192), (1, 0, 192), (2, 0, 192)),
-    2: ((0, 192, 384), (1, 192, 384), (2, 192, 384)),
-    4: ((0, 384, 576), (1, 384, 576), (2, 384, 640)),
-    5: ((0, 576, 768), (1, 576, 768)),
+    1: ((0, 0, 160), (1, 0, 160), (2, 0, 160)),
+    2: ((0, 160, 384), (1, 160, 320), (2, 160, 320)),
+    3: ((1, 320, 512), (2, 320, 512)),
+    4: ((0, 384, 608),),
 }
 LATE = E - 3
+X_BYTES = 4 * PACK * T
+W_BYTES = 4 * PACK * N
+RAW_AT = (5, 6, 7, 8, 0, 1, 2, 3, 4, 5, 6, 7, 0, 1)
+LANE = LATE * C + PACK * N
 
 
 def tile_moe_nxt_lin_none_kernel(tc, xT, w, wp, gate, offs, out):
     nc = tc.nc
     with ExitStack() as ctx:
         rows = ctx.enter_context(tc.tile_pool(name="rows", bufs=1))
-        wraw = ctx.enter_context(tc.tile_pool(name="wraw", bufs=5))
+        turns = ctx.enter_context(tc.tile_pool(name="turns", bufs=1))
         keep = ctx.enter_context(tc.tile_pool(name="keep", bufs=1))
         xbf = ctx.enter_context(tc.tile_pool(name="xbf", bufs=PASSES))
-        wbf = ctx.enter_context(tc.tile_pool(name="wbf", bufs=3))
+        wbf = ctx.enter_context(tc.tile_pool(name="wbf", bufs=2))
         wq = ctx.enter_context(tc.tile_pool(name="wq", bufs=3))
-        cq = ctx.enter_context(tc.tile_pool(name="cq", bufs=3))
+        cq = ctx.enter_context(tc.tile_pool(name="cq", bufs=1))
         psum = ctx.enter_context(tc.psum_pool(name="psum", bufs=8))
 
         offsets = keep.tile([P, SLOTS // 16], U16, name="offsets")
         xcodes = [keep.tile([P, T + a * SPARE], U32, align_bytes=64, name="xcodes%d" % a) for a in range(PASSES)]
         xscales = keep.tile([P, T + SPARE], U8, align_bytes=64, name="xscales")
         gcodes = [keep.tile([P, SLOTS], U32, align_bytes=64, name="gcodes%d" % a) for a in range(PASSES)]
-        gscales = keep.tile([P, SLOTS], U8, align_bytes=64, name="gscales")
+        gscales = keep.tile([P, LATE * C], U8, align_bytes=64, name="gscales")
         identity = keep.tile([P, P], F32, name="identity")
         gate_rows = keep.tile([P, C], F32, name="gate_rows")
         gate_columns = keep.tile([P, E], F32, name="gate_columns")
@@ -69,7 +77,9 @@ def tile_moe_nxt_lin_none_kernel(tc, xT, w, wp, gate, offs, out):
         wpcodes = keep.tile([P, M], U32, align_bytes=64, name="wpcodes")
         wpscales = keep.tile([P, M], U8, align_bytes=64, name="wpscales")
         windows = [rows.tile([P, T], F32, align_bytes=256, name="window%d" % f) for f in range(F_BLOCKS)]
-        staged = keep.tile([P, F_BLOCKS, (LATE + 1) * C], F32, name="staged")
+        lanes = rows.tile([P, F_BLOCKS * LANE], F32, align_bytes=256, name="lanes")
+        staged = lanes[:].rearrange("p (f s) -> p f s", f=F_BLOCKS)
+        slot_scales = [gscales[:, e * C:(e + 1) * C] for e in range(LATE)]
         zeros = keep.tile([P, C], F32, name="zeros")
 
         nc.vector.memset(xscales[:].bitcast(I32), 0)
@@ -89,7 +99,7 @@ def tile_moe_nxt_lin_none_kernel(tc, xT, w, wp, gate, offs, out):
 
         def quantize_x(a):
             xb = xbf.tile([P, T * PACK], BF16, align_bytes=64, name="xb")
-            xr = rows.tile([P, PACK * T], F32, align_bytes=256, name="xr%d" % a)
+            xr = turns.tile([P, PACK * T], F32, align_bytes=256, offset=a * X_BYTES, name="xr%d" % a)
             nc.sync.dma_start(xr[:], xT[a * KP:(a + 1) * KP, :].rearrange("(p j) t -> p (j t)", j=PACK))
             if a == 0:
                 nc.sync.dma_start(offsets[:], offs)
@@ -110,94 +120,122 @@ def tile_moe_nxt_lin_none_kernel(tc, xT, w, wp, gate, offs, out):
         def gather_codes(a, s0, s1):
             nc.vector.tensor_copy(out=gcodes[a][:, s0:s1], in_=xcodes[a][:].indirect(offsets_of(s0, s1)))
 
-        def gather_scales(s0, s1):
-            nc.vector.tensor_copy(out=gscales[:, s0:s1], in_=xscales[:].indirect(offsets_of(s0, s1)))
+        def gather_scales(dst, s0, s1):
+            nc.vector.tensor_copy(out=dst, in_=xscales[:].indirect(offsets_of(s0, s1)))
 
         def load_w(k):
             e, a = divmod(k, PASSES)
-            if k == CHUNKS - 1:
-                raw = rows.tile([P, PACK * N], F32, align_bytes=256, name="raw_last")
+            if k >= CHUNKS - PASSES:
+                raw = staged[:, a, LATE * C:]
             else:
-                raw = wraw.tile([P, PACK * N], F32, align_bytes=256, name="raw")
-            nc.sync.dma_start(raw[:], w[e, a * KP:(a + 1) * KP, :].rearrange("(p j) n -> p (j n)", j=PACK))
+                raw = turns.tile([P, PACK * N], F32, align_bytes=256, offset=RAW_AT[k] * W_BYTES, name="raw%d" % k)[:]
+            nc.sync.dma_start(raw, w[e, a * KP:(a + 1) * KP, :].rearrange("(p j) n -> p (j n)", j=PACK))
             return raw
 
+        def places(e):
+            if e == E - 1:
+                return slice(0, PACK), slice(PACK + 1, BLOCKS), PACK
+            return slice(2, BLOCKS, 2), slice(1, BLOCKS - 1, 2), 0
+
         def round_w(k, raw, dst):
-            src = raw[:].rearrange("p (j c t i) -> p c t j i", j=PACK, t=PACK, i=4)
+            src = raw.rearrange("p (j c t i) -> p c t j i", j=PACK, t=PACK, i=4)
             share = VECTOR_QUARTERS[k]
-            if share == PACK:
-                for t0 in (0, 2):
-                    copy("v", dst[:, :, t0:t0 + 2], src[:, :, t0:t0 + 2])
+            if k == CHUNKS - 2:
+                copy("s", dst[:, 0:P // 8], src[:, 0:P // 8])
+                copy("v", dst[:, P // 8:P // 4], src[:, P // 8:P // 4])
                 return
-            if share:
+            if share > 2 and k % PASSES:
+                copy("v", dst[:, :, 0:2], src[:, :, 0:2])
+                copy("v", dst[:, :, 2:share], src[:, :, 2:share])
+            elif share:
                 copy("v", dst[:, :, 0:share], src[:, :, 0:share])
-            copy("s", dst[:, :, share:PACK], src[:, :, share:PACK])
+            if share < PACK:
+                copy("s", dst[:, :, share:PACK], src[:, :, share:PACK])
 
-        def quantize_w(e, raws):
-            last = e == E - 1
-            order = "(a t" if last else "(t a"
-            grouped = wbf.tile([P, PASSES * N * PACK], BF16, align_bytes=64, name="grouped")
-            codes = wq.tile([P, PASSES * N], U32, align_bytes=64, name="codes")
-            scales = wq.tile([P, PASSES * N], U8, align_bytes=64, name="scales")
-            dst = grouped[:].rearrange("p " + order + " c i j) -> p a c t j i", a=PASSES, t=PACK, i=4, j=PACK)
-            width = N // 2 if last else N
+        def rounded_tile():
+            return wbf.tile([P, BLOCKS * P * PACK], BF16, align_bytes=64, name="grouped")
 
-            def quantize(n0):
+        def round_chunk(k, grouped):
+            e, a = divmod(k, PASSES)
+            raw = load_w(k)
+            dst = grouped[:].rearrange("p (b c i j) -> p c b j i", b=BLOCKS, i=4, j=PACK)
+            round_w(k, raw, dst[:, :, places(e)[a]])
+            return raw
+
+        def quantize(e, grouped):
+            codes = wq.tile([P, BLOCKS * P], U32, align_bytes=64, name="codes")
+            scales = wq.tile([P, BLOCKS * P], U8, align_bytes=64, name="scales")
+            for b0, b1 in CUTS_FIRST if e == 0 else CUTS_LAST if e == E - 1 else CUTS:
                 nc.vector.quantize_mx(
-                    out=codes[:, n0:n0 + width].bitcast(FP8X4),
-                    scales=scales[:, n0:n0 + width],
-                    in_=grouped[:, n0 * PACK:(n0 + width) * PACK],
+                    out=codes[:, b0 * P:b1 * P].bitcast(FP8X4),
+                    scales=scales[:, b0 * P:b1 * P],
+                    in_=grouped[:, b0 * P * PACK:b1 * P * PACK],
                 )
+            return codes[:].rearrange("p (b m) -> p b m", m=P), scales[:].rearrange("p (b m) -> p b m", m=P)
 
-            for a in range(PASSES):
-                round_w(e * PASSES + a, raws[a], dst[:, a])
-            for n0 in range(0, PASSES * N, width):
-                quantize(n0)
-            pattern = "p " + order + " m) -> p a t m"
-            return codes[:].rearrange(pattern, a=PASSES, t=PACK), scales[:].rearrange(pattern, a=PASSES, t=PACK)
-
-        def expert(e, quantized):
+        def multiply(e, quantized):
             cols = slice(e * C, (e + 1) * C)
             y = psum.tile([P, PACK, C], F32, name="bank")
             joined = e == E - 1
-            steps = [(a, t) for t in range(PACK) for a in range(PASSES)]
-            codes, scales = quantized
-            for a, t in sorted(steps) if joined else steps:
+            order = range(PASSES) if joined else range(PASSES - 1, -1, -1)
+            steps = [(a, t) for t in range(PACK) for a in order]
+            steps = sorted(steps) if joined else steps
+            for a, t in steps:
+                codes, scales = [operand[:, places(e)[a], :][:, t, :] for operand in quantized]
                 nc.tensor.matmul_mx(
                     out=y[:, t, :],
-                    lhsT=codes[:, a, t, :].bitcast(FP8X4),
-                    lhsT_scale=scales[:, a, t, :],
+                    lhsT=codes.bitcast(FP8X4),
+                    lhsT_scale=scales,
                     rhs=gcodes[a][:, cols].bitcast(FP8X4),
-                    rhs_scale=gscales[PACK * a:P, cols],
-                    start=(a == 0 and (t == 0 or not joined)),
-                    stop=(a == PASSES - 1 and (t == PACK - 1 or not joined)),
+                    rhs_scale=slot_scales[e][PACK * a:P],
+                    start=((a, t) == steps[0] if joined else a == order[0]),
+                    stop=((a, t) == steps[-1] if joined else a == order[-1]),
                 )
-            cb = cq.tile([P, C * PACK], BF16, align_bytes=64, name="cb")
+            return y
+
+        def gated(e, y, cb):
             nc.vector.tensor_tensor(
-                out=cb[:].rearrange("p (s t) -> p s t", t=PACK),
+                out=cb.rearrange("p (s t) -> p s t", t=PACK),
                 in0=y[:].rearrange("p t s -> p s t"),
                 in1=spread[:, e, :].unsqueeze(2).to_broadcast([P, C, PACK]),
                 op=MULT,
             )
-            ccodes = cq.tile([P, C], U32, align_bytes=64, name="ccodes")
-            cscales = cq.tile([P, C], U8, align_bytes=64, name="cscales")
-            nc.vector.quantize_mx(out=ccodes[:].bitcast(FP8X4), scales=cscales[:], in_=cb[:])
-            return ccodes, cscales
 
-        def project(f0, f1, quantized, dst, engine="s"):
+        def step(e, y):
+            grouped = rounded_tile()
+            at = places(e)[2]
+            round_chunk(e * PASSES, grouped)
+            gated(e - 1, y, grouped[:, at * C * PACK:(at + 1) * C * PACK])
+            raw = round_chunk(e * PASSES + 1, grouped)
+            codes, scales = quantize(e, grouped)
+            return (codes[:, at, :], scales[:, at, :]), (codes, scales), raw
+
+        def projection(dst, f, quantized):
             ccodes, cscales = quantized
-            bank = psum.tile([P, f1 - f0, C], F32, name="bank")
-            for f in range(f0, f1):
-                nc.tensor.matmul_mx(
-                    out=bank[:, f - f0, :],
-                    lhsT=wpcodes[:, f * P:(f + 1) * P].bitcast(FP8X4),
-                    lhsT_scale=wpscales[:, f * P:(f + 1) * P],
-                    rhs=ccodes[:].bitcast(FP8X4),
-                    rhs_scale=cscales[:],
-                    start=True,
-                    stop=True,
-                )
+            nc.tensor.matmul_mx(
+                out=dst,
+                lhsT=wpcodes[:, f * P:(f + 1) * P].bitcast(FP8X4),
+                lhsT_scale=wpscales[:, f * P:(f + 1) * P],
+                rhs=ccodes.bitcast(FP8X4),
+                rhs_scale=cscales,
+                start=True,
+                stop=True,
+            )
+
+        def project(features, quantized, dst, engine="s"):
+            bank = psum.tile([P, len(features), C], F32, name="bank")
+            for i, f in enumerate(features):
+                projection(bank[:, i, :], f, quantized)
             copy(engine, dst, bank[:])
+
+        def projected(blocks, pieces):
+            bank = psum.tile([P, len(blocks) * C], F32, name="bank")
+            for i, (f, quantized) in enumerate(blocks):
+                projection(bank[:, i * C:(i + 1) * C], f, quantized)
+            done = 0
+            for dst, count in pieces:
+                copy("s", dst, bank[:, done * C:(done + count) * C])
+                done = done + count
 
         def spread_gates():
             make_identity(nc, identity[:])
@@ -212,15 +250,15 @@ def tile_moe_nxt_lin_none_kernel(tc, xT, w, wp, gate, offs, out):
                     nc.tensor.transpose(bank[:, e - e0, :], gate_columns[:, e:e + 1].to_broadcast([P, P]), identity[:])
                 nc.scalar.copy(out=spread[:, e0:e0 + BANK // C, :], in_=bank[:])
 
-        def scatter_scalar(f, s0, s1, values):
-            nc.scalar.activation(windows[f][:].indirect(offsets_of(s0, s1)), values, COPY)
+        def scatter_scalar(f, s0, s1):
+            nc.scalar.activation(windows[f][:].indirect(offsets_of(s0, s1)), staged[:, f, s0:s1], COPY)
 
         def scatter_vector(f, e, values):
             nc.vector.tensor_tensor(
                 out=windows[f][:].indirect(offsets_of(e * C, (e + 1) * C)), in0=values, in1=zeros[:], op=ADD
             )
 
-        def quantize_wp():
+        def load_wp():
             blocks = wp.rearrange("(c t i) f -> t c i f", t=PACK, i=4)
             for t in range(PACK):
                 nc.sync.dma_start(wpraw[:, t, :], blocks[t])
@@ -229,6 +267,8 @@ def tile_moe_nxt_lin_none_kernel(tc, xT, w, wp, gate, offs, out):
                 wpbf[:].rearrange("q (c i) r -> q c r i", i=4),
                 wpraw[:].rearrange("q r (c i) -> q c r i", i=4),
             )
+
+        def quantize_wp():
             nc.vector.quantize_mx(
                 out=wpcodes[:].bitcast(FP8X4), scales=wpscales[:], in_=wpbf[:].rearrange("p f r -> p (f r)")
             )
@@ -242,33 +282,47 @@ def tile_moe_nxt_lin_none_kernel(tc, xT, w, wp, gate, offs, out):
             gather_codes(0, s0, s1)
         quantize_x(1)
         gather_codes(1, 0, SLOTS)
-        gather_scales(0, SLOTS)
+        gather_scales(gscales[:], 0, LATE * C)
+
+        grouped = rounded_tile()
+        for k in range(PASSES):
+            round_chunk(k, grouped)
+        y = multiply(0, quantize(0, grouped))
+        load_wp()
         quantize_wp()
-
-        def load_expert(e):
-            return [load_w(k) for k in range(e * PASSES, (e + 1) * PASSES)]
-
-        for e in range(LATE + 1):
-            c = expert(e, quantize_w(e, load_expert(e)))
-            early = F_BLOCKS if e < LATE else F_BLOCKS - 1
-            project(0, early, c, staged[:, 0:early, e * C:(e + 1) * C])
+        for e in range(E - 2):
+            c, quantized, raw = step(e + 1, y)
+            if e == 0:
+                late_scales = turns.tile([P, SLOTS - LATE * C], U8, align_bytes=256, offset=RAW_AT[3] * W_BYTES, name="late_scales")
+                gather_scales(late_scales[:], LATE * C, SLOTS)
+                slot_scales.extend(late_scales[:, i * C:(i + 1) * C] for i in range(E - LATE))
+            if e < LATE:
+                project(range(F_BLOCKS), c, staged[:, :, e * C:(e + 1) * C])
+            y = multiply(e + 1, quantized)
             for f, s0, s1 in EARLY_SCATTERS.get(e, ()):
-                scatter_scalar(f, s0, s1, staged[:, f, s0:s1])
+                scatter_scalar(f, s0, s1)
 
-        c6 = expert(E - 2, quantize_w(E - 2, load_expert(E - 2)))
-        raws = load_expert(E - 1)
-        quantized = quantize_w(E - 1, raws)
-        room = raws[-1][:, 0:F_BLOCKS * 3 * C].rearrange("p (f s) -> p f s", f=F_BLOCKS)
-        project(0, F_BLOCKS, c6, room[:, :, C:2 * C])
-        project(2, 3, c, room[:, 2:3, 0:C])
-        scatter_vector(0, E - 2, room[:, 0, C:2 * C])
-        scatter_scalar(2, LATE * C, (E - 1) * C, room[:, 2, 0:2 * C])
-        c7 = expert(E - 1, quantized)
-        project(0, 1, c7, room[:, 0:1, 2 * C:3 * C], "v")
-        project(1, F_BLOCKS, c7, room[:, 1:F_BLOCKS, 2 * C:3 * C])
-        scatter_vector(0, E - 1, room[:, 0, 2 * C:3 * C])
-        store(0)
-        scatter_scalar(1, (E - 2) * C, SLOTS, room[:, 1, C:3 * C])
-        store(1)
-        scatter_vector(2, E - 1, room[:, 2, 2 * C:3 * C])
-        store(2)
+        c5 = c
+        c6, quantized, raw = step(E - 1, y)
+        project((0,), c5, staged[:, 0:1, LATE * C:(LATE + 1) * C])
+        scatter_scalar(0, 608, 768)
+        projected(((1, c5), (1, c6)), ((staged[:, 1, LATE * C:(E - 1) * C], 2),))
+        y = multiply(E - 1, quantized)
+        scatter_scalar(1, 512, (E - 1) * C)
+        cb = cq.tile([P, C * PACK], BF16, align_bytes=64, name="cb")
+        gated(E - 1, y, cb[:])
+        ccodes = cq.tile([P, C], U32, align_bytes=64, name="ccodes")
+        cscales = cq.tile([P, C], U8, align_bytes=64, name="cscales")
+        nc.vector.quantize_mx(out=ccodes[:].bitcast(FP8X4), scales=cscales[:], in_=cb[:])
+        c7 = (ccodes[:], cscales[:])
+        project((0,), c6, spread[:, E - 1:E, :], "v")
+        project((0,), c7, staged[:, 0:1, (E - 1) * C:SLOTS])
+        projected(
+            ((2, c5), (2, c6), (2, c7), (1, c7)),
+            ((staged[:, 2, LATE * C:SLOTS], 3), (staged[:, 1, (E - 1) * C:SLOTS], 1)),
+        )
+        scatter_scalar(2, 512, (E - 1) * C)
+        scatter_vector(0, E - 2, spread[:, E - 1, :])
+        for f in range(F_BLOCKS):
+            scatter_vector(f, E - 1, staged[:, f, (E - 1) * C:SLOTS])
+            store(f)

@@ -31,23 +31,41 @@ X_COPIES = (
 )
 X_QUANTIZE = ((0, 512), (512, 768), (768, 1280))
 GATHERS = ((0, 512), (512, 1024))
-VECTOR_QUARTERS = (0, 0, 0, 2, 0, 2, 3, 4, 3, 4, 3, 3, 3, 3, 2, 2)
-BLOCKS = PASSES * PACK + 1
-CUTS_FIRST = ((1, 5), (5, 9))
-CUTS = ((0, 2), (2, 6), (6, 9))
-CUTS_LAST = ((0, 2), (2, 5), (5, 7), (7, 9))
+VECTOR_QUARTERS = (
+    (("s", 0, 4),),
+    (("s", 0, 4),),
+    (("s", 0, 4),),
+    (("v", 0, 2), ("s", 2, 4)),
+    (("s", 0, 4),),
+    (("v", 0, 2), ("v", 2, 4)),
+    (),
+    (("v", 0, 2), ("v", 2, 3), ("s", 3, 4)),
+    (),
+    (("v", 0, 2), ("v", 2, 3), ("s", 3, 4)),
+    (),
+    (("v", 0, 2), ("v", 2, 3), ("s", 3, 4)),
+    (),
+    (("v", 0, 2), ("v", 2, 3), ("s", 3, 4)),
+    (),
+    (("v", 0, 2), ("v", 2, 3), ("s", 3, 4)),
+)
+BLOCKS = PASSES * PACK
+PLAIN = ((0, 1, 2, 3), (4, 5, 6, 7), None, (0, 4, 6, 8))
+FIRST = ((0, 1, 2, 3), (4, 5, 6, 7), None, (0, 4, 8))
+LAYOUTS = (FIRST,) + (PLAIN,) * (E - 1)
+HELD_FROM = 3
 BANK = 512
 SPARE = 128
 EARLY_SCATTERS = {
-    1: ((0, 0, 160), (1, 0, 160), (2, 0, 160)),
-    2: ((0, 160, 384), (1, 160, 320), (2, 160, 320)),
-    3: ((1, 320, 512), (2, 320, 512)),
-    4: ((0, 384, 608),),
+    1: ((0, 0, 256), (1, 0, 192)),
+    2: ((2, 0, 288), (1, 192, 352)),
+    3: ((1, 352, 512), (2, 288, 448)),
+    4: ((0, 256, 608),),
 }
 LATE = E - 3
 X_BYTES = 4 * PACK * T
 W_BYTES = 4 * PACK * N
-RAW_AT = (5, 6, 7, 8, 0, 1, 2, 3, 4, 5, 6, 7, 0, 1)
+RAW_AT = (5, 6, 7, 8, None, 0, 1, 2, 3, 4, 5, 6, 7, 0)
 LANE = LATE * C + PACK * N
 
 
@@ -60,7 +78,7 @@ def tile_moe_nxt_lin_none_kernel(tc, xT, w, wp, gate, offs, out):
         xbf = ctx.enter_context(tc.tile_pool(name="xbf", bufs=PASSES))
         wbf = ctx.enter_context(tc.tile_pool(name="wbf", bufs=2))
         wq = ctx.enter_context(tc.tile_pool(name="wq", bufs=3))
-        cq = ctx.enter_context(tc.tile_pool(name="cq", bufs=1))
+        cq = ctx.enter_context(tc.tile_pool(name="cq", bufs=3))
         psum = ctx.enter_context(tc.psum_pool(name="psum", bufs=8))
 
         offsets = keep.tile([P, SLOTS // 16], U16, name="offsets")
@@ -127,69 +145,61 @@ def tile_moe_nxt_lin_none_kernel(tc, xT, w, wp, gate, offs, out):
             e, a = divmod(k, PASSES)
             if k >= CHUNKS - PASSES:
                 raw = staged[:, a, LATE * C:]
+            elif k == 4:
+                raw = staged[:, F_BLOCKS - 1, 0:PACK * N]
             else:
                 raw = turns.tile([P, PACK * N], F32, align_bytes=256, offset=RAW_AT[k] * W_BYTES, name="raw%d" % k)[:]
             nc.sync.dma_start(raw, w[e, a * KP:(a + 1) * KP, :].rearrange("(p j) n -> p (j n)", j=PACK))
             return raw
 
-        def places(e):
-            if e == E - 1:
-                return slice(0, PACK), slice(PACK + 1, BLOCKS), PACK
-            return slice(2, BLOCKS, 2), slice(1, BLOCKS - 1, 2), 0
-
-        def round_w(k, raw, dst):
-            src = raw.rearrange("p (j c t i) -> p c t j i", j=PACK, t=PACK, i=4)
-            share = VECTOR_QUARTERS[k]
-            if k == CHUNKS - 2:
-                copy("s", dst[:, 0:P // 8], src[:, 0:P // 8])
-                copy("v", dst[:, P // 8:P // 4], src[:, P // 8:P // 4])
-                return
-            if share > 2 and k % PASSES:
-                copy("v", dst[:, :, 0:2], src[:, :, 0:2])
-                copy("v", dst[:, :, 2:share], src[:, :, 2:share])
-            elif share:
-                copy("v", dst[:, :, 0:share], src[:, :, 0:share])
-            if share < PACK:
-                copy("s", dst[:, :, share:PACK], src[:, :, share:PACK])
-
-        def rounded_tile():
-            return wbf.tile([P, BLOCKS * P * PACK], BF16, align_bytes=64, name="grouped")
-
         def round_chunk(k, grouped):
             e, a = divmod(k, PASSES)
             raw = load_w(k)
+            src = raw.rearrange("p (j c t i) -> p c t j i", j=PACK, t=PACK, i=4)
             dst = grouped[:].rearrange("p (b c i j) -> p c b j i", b=BLOCKS, i=4, j=PACK)
-            round_w(k, raw, dst[:, :, places(e)[a]])
+            places = LAYOUTS[e][a]
+
+            def part(engine, t0, t1, columns=slice(0, P // 4)):
+                copy(engine, dst[:, columns, places[t0]:places[t0] + t1 - t0], src[:, columns, t0:t1])
+
+            if a == 0 and e >= HELD_FROM:
+                part("s" if e == E - 1 else "v", 0, PACK, slice(0, P // 8))
+                part("v", 0, PACK, slice(P // 8, P // 4))
+            for engine, t0, t1 in VECTOR_QUARTERS[k]:
+                part(engine, t0, t1)
             return raw
 
-        def quantize(e, grouped):
-            codes = wq.tile([P, BLOCKS * P], U32, align_bytes=64, name="codes")
-            scales = wq.tile([P, BLOCKS * P], U8, align_bytes=64, name="scales")
-            for b0, b1 in CUTS_FIRST if e == 0 else CUTS_LAST if e == E - 1 else CUTS:
+        def quantize(quantized, grouped, cuts):
+            codes, scales = quantized
+            for b0, b1 in zip(cuts, cuts[1:]):
                 nc.vector.quantize_mx(
-                    out=codes[:, b0 * P:b1 * P].bitcast(FP8X4),
-                    scales=scales[:, b0 * P:b1 * P],
+                    out=codes[:, b0:b1, :].rearrange("p b m -> p (b m)").bitcast(FP8X4),
+                    scales=scales[:, b0:b1, :].rearrange("p b m -> p (b m)"),
                     in_=grouped[:, b0 * P * PACK:b1 * P * PACK],
                 )
-            return codes[:].rearrange("p (b m) -> p b m", m=P), scales[:].rearrange("p (b m) -> p b m", m=P)
+
+        def quantize_c(cb):
+            ccodes = cq.tile([P, C], U32, align_bytes=64, name="ccodes")
+            cscales = cq.tile([P, C], U8, align_bytes=64, name="cscales")
+            nc.vector.quantize_mx(out=ccodes[:].bitcast(FP8X4), scales=cscales[:], in_=cb)
+            return ccodes[:], cscales[:]
 
         def multiply(e, quantized):
             cols = slice(e * C, (e + 1) * C)
             y = psum.tile([P, PACK, C], F32, name="bank")
             joined = e == E - 1
-            order = range(PASSES) if joined else range(PASSES - 1, -1, -1)
-            steps = [(a, t) for t in range(PACK) for a in order]
+            steps = [(a, t) for t in range(PACK) for a in range(PASSES)]
             steps = sorted(steps) if joined else steps
             for a, t in steps:
-                codes, scales = [operand[:, places(e)[a], :][:, t, :] for operand in quantized]
+                codes, scales = [operand[:, LAYOUTS[e][a][t], :] for operand in quantized]
                 nc.tensor.matmul_mx(
                     out=y[:, t, :],
                     lhsT=codes.bitcast(FP8X4),
                     lhsT_scale=scales,
                     rhs=gcodes[a][:, cols].bitcast(FP8X4),
                     rhs_scale=slot_scales[e][PACK * a:P],
-                    start=((a, t) == steps[0] if joined else a == order[0]),
-                    stop=((a, t) == steps[-1] if joined else a == order[-1]),
+                    start=((a, t) == steps[0] if joined else a == 0),
+                    stop=((a, t) == steps[-1] if joined else a == PASSES - 1),
                 )
             return y
 
@@ -202,13 +212,26 @@ def tile_moe_nxt_lin_none_kernel(tc, xT, w, wp, gate, offs, out):
             )
 
         def step(e, y):
-            grouped = rounded_tile()
-            at = places(e)[2]
-            round_chunk(e * PASSES, grouped)
-            gated(e - 1, y, grouped[:, at * C * PACK:(at + 1) * C * PACK])
-            raw = round_chunk(e * PASSES + 1, grouped)
-            codes, scales = quantize(e, grouped)
-            return (codes[:, at, :], scales[:, at, :]), (codes, scales), raw
+            grouped = wbf.tile([P, BLOCKS * P * PACK], BF16, align_bytes=64, name="grouped")
+            codes = wq.tile([P, BLOCKS, P], U32, align_bytes=64, name="codes")
+            scales = wq.tile([P, BLOCKS, P], U8, align_bytes=64, name="scales")
+            at, cuts = LAYOUTS[e][2:]
+            raw = round_chunk(e * PASSES, grouped)
+            c = None
+            if e == E - 1:
+                cb = raw[:, N // 2:N].bitcast(BF16)
+            elif e >= HELD_FROM:
+                cb = raw[:, 0:C * PACK // 2].bitcast(BF16)
+            elif e:
+                cb = cq.tile([P, C * PACK], BF16, align_bytes=64, name="cb")[:]
+            if e:
+                gated(e - 1, y, cb)
+            quantize((codes, scales), grouped, cuts[0:2])
+            if e:
+                c = quantize_c(cb)
+            round_chunk(e * PASSES + 1, grouped)
+            quantize((codes, scales), grouped, cuts[1:])
+            return (codes, scales), c
 
         def projection(dst, f, quantized):
             ccodes, cscales = quantized
@@ -234,7 +257,8 @@ def tile_moe_nxt_lin_none_kernel(tc, xT, w, wp, gate, offs, out):
                 projection(bank[:, i * C:(i + 1) * C], f, quantized)
             done = 0
             for dst, count in pieces:
-                copy("s", dst, bank[:, done * C:(done + count) * C])
+                src = bank[:, done * C:(done + count) * C]
+                copy("s", dst, src if dst.ndim == 2 else src.rearrange("p (f s) -> p f s", s=C))
                 done = done + count
 
         def spread_gates():
@@ -284,45 +308,45 @@ def tile_moe_nxt_lin_none_kernel(tc, xT, w, wp, gate, offs, out):
         gather_codes(1, 0, SLOTS)
         gather_scales(gscales[:], 0, LATE * C)
 
-        grouped = rounded_tile()
-        for k in range(PASSES):
-            round_chunk(k, grouped)
-        y = multiply(0, quantize(0, grouped))
+        y = multiply(0, step(0, None)[0])
         load_wp()
         quantize_wp()
         for e in range(E - 2):
-            c, quantized, raw = step(e + 1, y)
+            quantized, c = step(e + 1, y)
             if e == 0:
                 late_scales = turns.tile([P, SLOTS - LATE * C], U8, align_bytes=256, offset=RAW_AT[3] * W_BYTES, name="late_scales")
                 gather_scales(late_scales[:], LATE * C, SLOTS)
                 slot_scales.extend(late_scales[:, i * C:(i + 1) * C] for i in range(E - LATE))
-            if e < LATE:
+            if e == 1:
+                project(range(F_BLOCKS), c0, staged[:, :, 0:C])
+            if e == 0:
+                c0 = c
+            elif e < LATE:
                 project(range(F_BLOCKS), c, staged[:, :, e * C:(e + 1) * C])
             y = multiply(e + 1, quantized)
             for f, s0, s1 in EARLY_SCATTERS.get(e, ()):
                 scatter_scalar(f, s0, s1)
 
         c5 = c
-        c6, quantized, raw = step(E - 1, y)
+        quantized, c6 = step(E - 1, y)
         project((0,), c5, staged[:, 0:1, LATE * C:(LATE + 1) * C])
         scatter_scalar(0, 608, 768)
-        projected(((1, c5), (1, c6)), ((staged[:, 1, LATE * C:(E - 1) * C], 2),))
+        first6 = staged[:, 1, SLOTS:SLOTS + C]
+        projected(((0, c6), (1, c5), (1, c6)), ((first6, 1), (staged[:, 1, LATE * C:(E - 1) * C], 2)))
         y = multiply(E - 1, quantized)
+        scatter_vector(0, E - 2, first6)
         scatter_scalar(1, 512, (E - 1) * C)
         cb = cq.tile([P, C * PACK], BF16, align_bytes=64, name="cb")
         gated(E - 1, y, cb[:])
-        ccodes = cq.tile([P, C], U32, align_bytes=64, name="ccodes")
-        cscales = cq.tile([P, C], U8, align_bytes=64, name="cscales")
-        nc.vector.quantize_mx(out=ccodes[:].bitcast(FP8X4), scales=cscales[:], in_=cb[:])
-        c7 = (ccodes[:], cscales[:])
-        project((0,), c6, spread[:, E - 1:E, :], "v")
+        c7 = quantize_c(cb[:])
+        project((2,), c6, spread[:, E - 1:E, :], "v")
+        scatter_vector(2, E - 2, spread[:, E - 1, :])
         project((0,), c7, staged[:, 0:1, (E - 1) * C:SLOTS])
         projected(
-            ((2, c5), (2, c6), (2, c7), (1, c7)),
-            ((staged[:, 2, LATE * C:SLOTS], 3), (staged[:, 1, (E - 1) * C:SLOTS], 1)),
+            ((1, c7), (2, c7), (2, c5)),
+            ((staged[:, 1:F_BLOCKS, (E - 1) * C:SLOTS], 2), (staged[:, 2, LATE * C:(LATE + 1) * C], 1)),
         )
-        scatter_scalar(2, 512, (E - 1) * C)
-        scatter_vector(0, E - 2, spread[:, E - 1, :])
+        scatter_scalar(2, 448, (E - 2) * C)
         for f in range(F_BLOCKS):
             scatter_vector(f, E - 1, staged[:, f, (E - 1) * C:SLOTS])
             store(f)

@@ -59,8 +59,8 @@ SPARE = 128
 EARLY_SCATTERS = {
     1: ((0, 0, 256), (1, 0, 192)),
     2: ((2, 0, 288), (1, 192, 352)),
-    3: ((1, 352, 512), (2, 288, 448)),
-    4: ((0, 256, 608),),
+    3: ((2, 288, 512), (0, 256, 448)),
+    4: ((1, 352, 608), (0, 448, 608)),
 }
 LATE = E - 3
 X_BYTES = 4 * PACK * T
@@ -162,8 +162,12 @@ def tile_moe_nxt_lin_none_kernel(tc, xT, w, wp, gate, offs, out):
             def part(engine, t0, t1, columns=slice(0, P // 4)):
                 copy(engine, dst[:, columns, places[t0]:places[t0] + t1 - t0], src[:, columns, t0:t1])
 
-            if a == 0 and e >= HELD_FROM:
-                part("s" if e == E - 1 else "v", 0, PACK, slice(0, P // 8))
+            if k == CHUNKS - 2:
+                part("s", 0, PACK, slice(0, 12))
+                part("v", 0, PACK, slice(16, P // 4))
+                part("v", 0, PACK, slice(12, 16))
+            elif a == 0 and e >= HELD_FROM:
+                part("v", 0, PACK, slice(0, P // 8))
                 part("v", 0, PACK, slice(P // 8, P // 4))
             for engine, t0, t1 in VECTOR_QUARTERS[k]:
                 part(engine, t0, t1)
@@ -335,7 +339,7 @@ def tile_moe_nxt_lin_none_kernel(tc, xT, w, wp, gate, offs, out):
         projected(((0, c6), (1, c5), (1, c6)), ((first6, 1), (staged[:, 1, LATE * C:(E - 1) * C], 2)))
         y = multiply(E - 1, quantized)
         scatter_vector(0, E - 2, first6)
-        scatter_scalar(1, 512, (E - 1) * C)
+        scatter_scalar(1, 608, (E - 1) * C)
         cb = cq.tile([P, C * PACK], BF16, align_bytes=64, name="cb")
         gated(E - 1, y, cb[:])
         c7 = quantize_c(cb[:])
@@ -346,7 +350,7 @@ def tile_moe_nxt_lin_none_kernel(tc, xT, w, wp, gate, offs, out):
             ((1, c7), (2, c7), (2, c5)),
             ((staged[:, 1:F_BLOCKS, (E - 1) * C:SLOTS], 2), (staged[:, 2, LATE * C:(LATE + 1) * C], 1)),
         )
-        scatter_scalar(2, 448, (E - 2) * C)
+        scatter_scalar(2, 512, (E - 2) * C)
         for f in range(F_BLOCKS):
             scatter_vector(f, E - 1, staged[:, f, (E - 1) * C:SLOTS])
             store(f)

@@ -27,9 +27,9 @@ CHUNKS = E * PASSES
 F_BLOCKS = M // P
 X_COPIES = (
     ((0, 512, "v"), (640, 768, "s"), (768, 1280, "s"), (512, 640, "v")),
-    ((0, 512, "v"), (768, 1280, "s"), (512, 768, "v")),
+    ((0, 512, "v"), (640, 768, "s"), (768, 1024, "s"), (1024, 1280, "s"), (512, 640, "v")),
 )
-X_QUANTIZE = ((0, 512), (512, 768), (768, 1280))
+X_QUANTIZE = (((0, 512), (512, 768), (768, 1280)), ((0, 512), (512, 768), (768, 1024), (1024, 1280)))
 GATHERS = ((0, 512), (512, 1024))
 VECTOR_QUARTERS = (
     (("s", 0, 4),),
@@ -37,7 +37,7 @@ VECTOR_QUARTERS = (
     (("s", 0, 4),),
     (("v", 0, 2), ("s", 2, 4)),
     (("s", 0, 4),),
-    (("v", 0, 2), ("v", 2, 4)),
+    (("v", 0, 2), ("v", 2, 3), ("s", 3, 4)),
     (),
     (("v", 0, 2), ("v", 2, 3), ("s", 3, 4)),
     (),
@@ -60,7 +60,7 @@ EARLY_SCATTERS = {
     1: ((0, 0, 256), (1, 0, 192)),
     2: ((2, 0, 288), (1, 192, 352)),
     3: ((2, 288, 512), (0, 256, 448)),
-    4: ((1, 352, 608), (0, 448, 608)),
+    4: ((1, 352, 640), (0, 448, 608)),
 }
 LATE = E - 3
 X_BYTES = 4 * PACK * T
@@ -128,7 +128,7 @@ def tile_moe_nxt_lin_none_kernel(tc, xT, w, wp, gate, offs, out):
                     xb[:, t0 * PACK:t1 * PACK].rearrange("p (c i j) -> p c j i", i=4, j=PACK),
                     lines[:, :, t0:t1].rearrange("p j (c i) -> p c j i", i=4),
                 )
-            for q0, q1 in X_QUANTIZE:
+            for q0, q1 in X_QUANTIZE[a]:
                 nc.vector.quantize_mx(
                     out=xcodes[a][:, q0:q1].bitcast(FP8X4),
                     scales=xscales[PACK * a:P, q0:q1],
@@ -339,7 +339,7 @@ def tile_moe_nxt_lin_none_kernel(tc, xT, w, wp, gate, offs, out):
         projected(((0, c6), (1, c5), (1, c6)), ((first6, 1), (staged[:, 1, LATE * C:(E - 1) * C], 2)))
         y = multiply(E - 1, quantized)
         scatter_vector(0, E - 2, first6)
-        scatter_scalar(1, 608, (E - 1) * C)
+        scatter_scalar(1, 640, (E - 1) * C)
         cb = cq.tile([P, C * PACK], BF16, align_bytes=64, name="cb")
         gated(E - 1, y, cb[:])
         c7 = quantize_c(cb[:])

from contextlib import ExitStack

import concourse.mybir as mybir
from concourse.masks import make_identity

K, T, E, C, N, M = 1024, 1280, 8, 128, 512, 384
SLOTS = E * C
FLOPS = 2 * SLOTS * K * N + 2 * T * N * M
BYTES = 4 * (K * T + E * K * N + N * M + SLOTS + M * T) + 2 * SLOTS

F32 = mybir.dt.float32
BF16 = mybir.dt.bfloat16
I32 = mybir.dt.int32
U32 = mybir.dt.uint32
U16 = mybir.dt.uint16
U8 = mybir.dt.uint8
FP8X4 = mybir.dt.float8_e4m3fn_x4
ADD = mybir.AluOpType.add
MULT = mybir.AluOpType.mult
COPY = mybir.ActivationFunctionType.Copy

P = 128
PACK = 4
KP = P * PACK
PASSES = K // KP
CHUNKS = E * PASSES
F_BLOCKS = M // P
X_COPIES = (
    ((0, 512, "v"), (640, 768, "s"), (768, 1280, "s"), (512, 640, "v")),
    ((0, 512, "v"), (640, 768, "s"), (768, 1024, "s"), (1024, 1280, "s"), (512, 640, "v")),
)
X_QUANTIZE = (((0, 512), (512, 768), (768, 1280)), ((0, 512), (512, 768), (768, 1024), (1024, 1280)))
GATHERS = ((0, 512), (512, 1024))
VECTOR_QUARTERS = (
    (("s", 0, 4),),
    (("s", 0, 4),),
    (("s", 0, 4),),
    (("v", 0, 2), ("s", 2, 4)),
    (("s", 0, 4),),
    (("v", 0, 2), ("v", 2, 3), ("s", 3, 4)),
    (),
    (("v", 0, 2), ("v", 2, 3), ("s", 3, 4)),
    (),
    (("v", 0, 2), ("v", 2, 3), ("s", 3, 4)),
    (),
    (("v", 0, 2), ("v", 2, 3), ("s", 3, 4)),
    (),
    (("v", 0, 2), ("v", 2, 3), ("s", 3, 4)),
    (),
    (("v", 0, 2), ("v", 2, 3), ("s", 3, 4)),
)
BLOCKS = PASSES * PACK
PLAIN = ((0, 1, 2, 3), (4, 5, 6, 7), None, (0, 4, 6, 8))
FIRST = ((0, 1, 2, 3), (4, 5, 6, 7), None, (0, 4, 8))
LAYOUTS = (FIRST,) + (PLAIN,) * (E - 1)
HELD_FROM = 3
BANK = 512
SPARE = 128
EARLY_SCATTERS = {
    1: ((0, 0, 256), (1, 0, 192)),
    2: ((2, 0, 288), (1, 192, 352)),
    3: ((2, 288, 512), (0, 256, 448)),
    4: ((1, 352, 640), (0, 448, 608)),
}
LATE = E - 3
X_BYTES = 4 * PACK * T
W_BYTES = 4 * PACK * N
RAW_AT = (5, 6, 7, 8, None, 0, 1, 2, 3, 4, 5, 6, 7, 0)
LANE = LATE * C + PACK * N


def tile_moe_nxt_lin_none_kernel(tc, xT, w, wp, gate, offs, out):
    nc = tc.nc
    with ExitStack() as ctx:
        rows = ctx.enter_context(tc.tile_pool(name="rows", bufs=1))
        turns = ctx.enter_context(tc.tile_pool(name="turns", bufs=1))
        keep = ctx.enter_context(tc.tile_pool(name="keep", bufs=1))
        xbf = ctx.enter_context(tc.tile_pool(name="xbf", bufs=PASSES))
        wbf = ctx.enter_context(tc.tile_pool(name="wbf", bufs=2))
        wq = ctx.enter_context(tc.tile_pool(name="wq", bufs=3))
        cq = ctx.enter_context(tc.tile_pool(name="cq", bufs=3))
        psum = ctx.enter_context(tc.psum_pool(name="psum", bufs=8))

        offsets = keep.tile([P, SLOTS // 16], U16, name="offsets")
        xcodes = [keep.tile([P, T + a * SPARE], U32, align_bytes=64, name="xcodes%d" % a) for a in range(PASSES)]
        xscales = keep.tile([P, T + SPARE], U8, align_bytes=64, name="xscales")
        gcodes = [keep.tile([P, SLOTS], U32, align_bytes=64, name="gcodes%d" % a) for a in range(PASSES)]
        gscales = keep.tile([P, LATE * C], U8, align_bytes=64, name="gscales")
        identity = keep.tile([P, P], F32, name="identity")
        gate_rows = keep.tile([P, C], F32, name="gate_rows")
        gate_columns = keep.tile([P, E], F32, name="gate_columns")
        spread = keep.tile([P, E, C], F32, name="spread")
        wpraw = rows.tile([P, PACK, M], F32, align_bytes=256, name="wpraw")
        wpbf = keep.tile([P, M, PACK], BF16, align_bytes=64, name="wpbf")
        wpcodes = keep.tile([P, M], U32, align_bytes=64, name="wpcodes")
        wpscales = keep.tile([P, M], U8, align_bytes=64, name="wpscales")
        windows = [rows.tile([P, T], F32, align_bytes=256, name="window%d" % f) for f in range(F_BLOCKS)]
        lanes = rows.tile([P, F_BLOCKS * LANE], F32, align_bytes=256, name="lanes")
        staged = lanes[:].rearrange("p (f s) -> p f s", f=F_BLOCKS)
        slot_scales = [gscales[:, e * C:(e + 1) * C] for e in range(LATE)]
        zeros = keep.tile([P, C], F32, name="zeros")

        nc.vector.memset(xscales[:].bitcast(I32), 0)
        nc.vector.memset(xcodes[1][:, T:].bitcast(I32), 0)
        nc.vector.memset(zeros[:], 0.0)
        for f in range(F_BLOCKS):
            nc.vector.memset(windows[f][:], 0.0)

        def copy(engine, dst, src):
            if engine == "v":
                nc.vector.tensor_copy(out=dst, in_=src)
            else:
                nc.scalar.copy(out=dst, in_=src)

        def offsets_of(s0, s1):
            return offsets[:, s0 // 16:s1 // 16]

        def quantize_x(a):
            xb = xbf.tile([P, T * PACK], BF16, align_bytes=64, name="xb")
            xr = turns.tile([P, PACK * T], F32, align_bytes=256, offset=a * X_BYTES, name="xr%d" % a)
            nc.sync.dma_start(xr[:], xT[a * KP:(a + 1) * KP, :].rearrange("(p j) t -> p (j t)", j=PACK))
            if a == 0:
                nc.sync.dma_start(offsets[:], offs)
            lines = xr[:].rearrange("p (j t) -> p j t", j=PACK)
            for t0, t1, engine in X_COPIES[a]:
                copy(
                    engine,
                    xb[:, t0 * PACK:t1 * PACK].rearrange("p (c i j) -> p c j i", i=4, j=PACK),
                    lines[:, :, t0:t1].rearrange("p j (c i) -> p c j i", i=4),
                )
            for q0, q1 in X_QUANTIZE[a]:
                nc.vector.quantize_mx(
                    out=xcodes[a][:, q0:q1].bitcast(FP8X4),
                    scales=xscales[PACK * a:P, q0:q1],
                    in_=xb[:, q0 * PACK:q1 * PACK],
                )

        def gather_codes(a, s0, s1):
            nc.vector.tensor_copy(out=gcodes[a][:, s0:s1], in_=xcodes[a][:].indirect(offsets_of(s0, s1)))

        def gather_scales(dst, s0, s1):
            nc.vector.tensor_copy(out=dst, in_=xscales[:].indirect(offsets_of(s0, s1)))

        def load_w(k):
            e, a = divmod(k, PASSES)
            if k >= CHUNKS - PASSES:
                raw = staged[:, a, LATE * C:]
            elif k == 4:
                raw = staged[:, F_BLOCKS - 1, 0:PACK * N]
            else:
                raw = turns.tile([P, PACK * N], F32, align_bytes=256, offset=RAW_AT[k] * W_BYTES, name="raw%d" % k)[:]
            nc.sync.dma_start(raw, w[e, a * KP:(a + 1) * KP, :].rearrange("(p j) n -> p (j n)", j=PACK))
            return raw

        def round_chunk(k, grouped):
            e, a = divmod(k, PASSES)
            raw = load_w(k)
            src = raw.rearrange("p (j c t i) -> p c t j i", j=PACK, t=PACK, i=4)
            dst = grouped[:].rearrange("p (b c i j) -> p c b j i", b=BLOCKS, i=4, j=PACK)
            places = LAYOUTS[e][a]

            def part(engine, t0, t1, columns=slice(0, P // 4)):
                copy(engine, dst[:, columns, places[t0]:places[t0] + t1 - t0], src[:, columns, t0:t1])

            if k == CHUNKS - 2:
                part("s", 0, PACK, slice(0, 12))
                part("v", 0, PACK, slice(16, P // 4))
                part("v", 0, PACK, slice(12, 16))
            elif a == 0 and e >= HELD_FROM:
                part("v", 0, PACK, slice(0, P // 8))
                part("v", 0, PACK, slice(P // 8, P // 4))
            for engine, t0, t1 in VECTOR_QUARTERS[k]:
                part(engine, t0, t1)
            return raw

        def quantize(quantized, grouped, cuts):
            codes, scales = quantized
            for b0, b1 in zip(cuts, cuts[1:]):
                nc.vector.quantize_mx(
                    out=codes[:, b0:b1, :].rearrange("p b m -> p (b m)").bitcast(FP8X4),
                    scales=scales[:, b0:b1, :].rearrange("p b m -> p (b m)"),
                    in_=grouped[:, b0 * P * PACK:b1 * P * PACK],
                )

        def quantize_c(cb):
            ccodes = cq.tile([P, C], U32, align_bytes=64, name="ccodes")
            cscales = cq.tile([P, C], U8, align_bytes=64, name="cscales")
            nc.vector.quantize_mx(out=ccodes[:].bitcast(FP8X4), scales=cscales[:], in_=cb)
            return ccodes[:], cscales[:]

        def multiply(e, quantized):
            cols = slice(e * C, (e + 1) * C)
            y = psum.tile([P, PACK, C], F32, name="bank")
            joined = e == E - 1
            steps = [(a, t) for t in range(PACK) for a in range(PASSES)]
            steps = sorted(steps) if joined else steps
            for a, t in steps:
                codes, scales = [operand[:, LAYOUTS[e][a][t], :] for operand in quantized]
                nc.tensor.matmul_mx(
                    out=y[:, t, :],
                    lhsT=codes.bitcast(FP8X4),
                    lhsT_scale=scales,
                    rhs=gcodes[a][:, cols].bitcast(FP8X4),
                    rhs_scale=slot_scales[e][PACK * a:P],
                    start=((a, t) == steps[0] if joined else a == 0),
                    stop=((a, t) == steps[-1] if joined else a == PASSES - 1),
                )
            return y

        def gated(e, y, cb):
            nc.vector.tensor_tensor(
                out=cb.rearrange("p (s t) -> p s t", t=PACK),
                in0=y[:].rearrange("p t s -> p s t"),
                in1=spread[:, e, :].unsqueeze(2).to_broadcast([P, C, PACK]),
                op=MULT,
            )

        def step(e, y):
            grouped = wbf.tile([P, BLOCKS * P * PACK], BF16, align_bytes=64, name="grouped")
            codes = wq.tile([P, BLOCKS, P], U32, align_bytes=64, name="codes")
            scales = wq.tile([P, BLOCKS, P], U8, align_bytes=64, name="scales")
            at, cuts = LAYOUTS[e][2:]
            raw = round_chunk(e * PASSES, grouped)
            c = None
            if e == E - 1:
                cb = raw[:, N // 2:N].bitcast(BF16)
            elif e >= HELD_FROM:
                cb = raw[:, 0:C * PACK // 2].bitcast(BF16)
            elif e:
                cb = cq.tile([P, C * PACK], BF16, align_bytes=64, name="cb")[:]
            if e:
                gated(e - 1, y, cb)
            quantize((codes, scales), grouped, cuts[0:2])
            if e:
                c = quantize_c(cb)
            round_chunk(e * PASSES + 1, grouped)
            quantize((codes, scales), grouped, cuts[1:])
            return (codes, scales), c

        def projection(dst, f, quantized):
            ccodes, cscales = quantized
            nc.tensor.matmul_mx(
                out=dst,
                lhsT=wpcodes[:, f * P:(f + 1) * P].bitcast(FP8X4),
                lhsT_scale=wpscales[:, f * P:(f + 1) * P],
                rhs=ccodes.bitcast(FP8X4),
                rhs_scale=cscales,
                start=True,
                stop=True,
            )

        def project(features, quantized, dst, engine="s"):
            bank = psum.tile([P, len(features), C], F32, name="bank")
            for i, f in enumerate(features):
                projection(bank[:, i, :], f, quantized)
            copy(engine, dst, bank[:])

        def projected(blocks, pieces):
            bank = psum.tile([P, len(blocks) * C], F32, name="bank")
            for i, (f, quantized) in enumerate(blocks):
                projection(bank[:, i * C:(i + 1) * C], f, quantized)
            done = 0
            for dst, count in pieces:
                src = bank[:, done * C:(done + count) * C]
                copy("s", dst, src if dst.ndim == 2 else src.rearrange("p (f s) -> p f s", s=C))
                done = done + count

        def spread_gates():
            make_identity(nc, identity[:])
            nc.gpsimd.memset(gate_rows[:], 0.0)
            nc.sync.dma_start(gate_rows[0:E, :], gate[0, :].rearrange("(e s) -> e s", s=C))
            turned = psum.tile([P, P], F32, name="bank")
            nc.tensor.transpose(turned[:], gate_rows[:], identity[:])
            nc.scalar.activation(gate_columns[:], turned[:, 0:E], COPY)
            for e0 in range(0, E, BANK // C):
                bank = psum.tile([P, BANK // C, C], F32, name="bank")
                for e in range(e0, e0 + BANK // C):
                    nc.tensor.transpose(bank[:, e - e0, :], gate_columns[:, e:e + 1].to_broadcast([P, P]), identity[:])
                nc.scalar.copy(out=spread[:, e0:e0 + BANK // C, :], in_=bank[:])

        def scatter_scalar(f, s0, s1):
            nc.scalar.activation(windows[f][:].indirect(offsets_of(s0, s1)), staged[:, f, s0:s1], COPY)

        def scatter_vector(f, e, values):
            nc.vector.tensor_tensor(
                out=windows[f][:].indirect(offsets_of(e * C, (e + 1) * C)), in0=values, in1=zeros[:], op=ADD
            )

        def load_wp():
            blocks = wp.rearrange("(c t i) f -> t c i f", t=PACK, i=4)
            for t in range(PACK):
                nc.sync.dma_start(wpraw[:, t, :], blocks[t])
            copy(
                "s",
                wpbf[:].rearrange("q (c i) r -> q c r i", i=4),
                wpraw[:].rearrange("q r (c i) -> q c r i", i=4),
            )

        def quantize_wp():
            nc.vector.quantize_mx(
                out=wpcodes[:].bitcast(FP8X4), scales=wpscales[:], in_=wpbf[:].rearrange("p f r -> p (f r)")
            )

        def store(f):
            nc.sync.dma_start(out[f * P:(f + 1) * P, :], windows[f][:])

        spread_gates()
        quantize_x(0)
        for s0, s1 in GATHERS:
            gather_codes(0, s0, s1)
        quantize_x(1)
        gather_codes(1, 0, SLOTS)
        gather_scales(gscales[:], 0, LATE * C)

        y = multiply(0, step(0, None)[0])
        load_wp()
        quantize_wp()
        for e in range(E - 2):
            quantized, c = step(e + 1, y)
            if e == 0:
                late_scales = turns.tile([P, SLOTS - LATE * C], U8, align_bytes=256, offset=RAW_AT[3] * W_BYTES, name="late_scales")
                gather_scales(late_scales[:], LATE * C, SLOTS)
                slot_scales.extend(late_scales[:, i * C:(i + 1) * C] for i in range(E - LATE))
            if e == 1:
                project(range(F_BLOCKS), c0, staged[:, :, 0:C])
            if e == 0:
                c0 = c
            elif e < LATE:
                project(range(F_BLOCKS), c, staged[:, :, e * C:(e + 1) * C])
            y = multiply(e + 1, quantized)
            for f, s0, s1 in EARLY_SCATTERS.get(e, ()):
                scatter_scalar(f, s0, s1)

        c5 = c
        quantized, c6 = step(E - 1, y)
        project((0,), c5, staged[:, 0:1, LATE * C:(LATE + 1) * C])
        scatter_scalar(0, 608, 768)
        first6 = staged[:, 1, SLOTS:SLOTS + C]
        projected(((0, c6), (1, c5), (1, c6)), ((first6, 1), (staged[:, 1, LATE * C:(E - 1) * C], 2)))
        y = multiply(E - 1, quantized)
        scatter_vector(0, E - 2, first6)
        scatter_scalar(1, 640, (E - 1) * C)
        cb = cq.tile([P, C * PACK], BF16, align_bytes=64, name="cb")
        gated(E - 1, y, cb[:])
        c7 = quantize_c(cb[:])
        project((2,), c6, spread[:, E - 1:E, :], "v")
        scatter_vector(2, E - 2, spread[:, E - 1, :])
        project((0,), c7, staged[:, 0:1, (E - 1) * C:SLOTS])
        projected(
            ((1, c7), (2, c7), (2, c5)),
            ((staged[:, 1:F_BLOCKS, (E - 1) * C:SLOTS], 2), (staged[:, 2, LATE * C:(LATE + 1) * C], 1)),
        )
        scatter_scalar(2, 512, (E - 2) * C)
        for f in range(F_BLOCKS):
            scatter_vector(f, E - 1, staged[:, f, (E - 1) * C:SLOTS])
            store(f)
